import numpy as np, ml_dtypes
CORES = [16,18,20,22]
N = 4
import mx_ref
BF = ml_dtypes.bfloat16
def pick(q, e):
    c = np.concatenate([q[0].reshape(128, -1, 4), np.zeros((128, 1, 4), np.uint8)], axis=1); s = np.concatenate([q[1], np.ones((16, 1), np.uint8)], axis=1)
    return (np.ascontiguousarray(c[:, e].reshape(128, -1)), np.ascontiguousarray(s[:, e]))
def join(*qs):
    return (np.concatenate([q[0] for q in qs], axis=1), np.concatenate([q[1] for q in qs], axis=1))
def put(q, e, v):
    c, s = q[0].reshape(128, -1, 4).copy(), q[1].copy(); c[:, e] = v[0].reshape(128, -1, 4); s[:, e] = v[1]
    return (c.reshape(128, -1), s)
def pk(c, s):
    return (np.ascontiguousarray(c), mx_ref.live(s))
def emit(q):
    return q[0], q[1]
def decode(q):
    o = []
    for b in range(4):
        e = np.zeros((128, 128, 4), np.float32); e[np.arange(128), np.arange(128), b] = 1
        o.append(mx_ref.matmul(mx_ref.quantize(e.reshape(128, 512).astype(BF)), q))
    return np.stack(o, axis=2).reshape(128, -1)
def cut(t, i, w=512):
    return t[:, w * i:w * i + w]
def f(rng, *shape):
    return mx_ref.flush((rng.standard_normal(shape, dtype=np.float32) * np.exp2(rng.integers(-2, 3, shape[:-1] + (1,)))).astype(BF))
def wide(rng, *shape, cols=0):
    v = rng.standard_normal(shape, dtype=np.float32) * np.exp2(rng.integers(-12, 13, shape)).astype(np.float32)
    if cols: v *= np.repeat(np.exp2(rng.integers(-cols, cols + 1, shape[:-2] + (1, shape[-1] // 4))) * (rng.random(shape[:-2] + (1, shape[-1] // 4)) > 0.0625), 4, axis=-1).astype(np.float32)
    return mx_ref.flush(v.astype(BF))
C, T, M, R, G, O = 32, 256, 12, 3, 3, 3
def big(v):
    v = v.astype(np.float32)
    return np.where(np.abs(v) < np.float32(2.0 ** -16), np.float32(0), v).astype(BF)
def signed(rng, *shape):
    return (1 + rng.random(shape)) * rng.choice([-1.0, 1.0], shape)
def tiles(v):
    return np.ascontiguousarray(v.reshape(N, 128, -1).astype(np.float32).astype(BF))
def setup_inputs(rng):
    return {"c": big(f(rng, N, 128, 4 * C)), "x": big(f(rng, N, 128, 4 * T)), "u": f(rng, N, 128, 16), "w": f(rng, N, 128, 512 * O)}
def setup_inputs_dark(rng):
    d = setup_inputs(rng)
    top = np.arange(128) < 64
    kind = np.stack([rng.permutation(T) for r in range(N)]) < 2 * T // 3
    on = kind[:, None, :] == top[None, :, None]
    d["x"] = tiles((1.75 + 0.25 * rng.random((N, 128, T, 4))) * on[:, :, :, None] * 2.0 ** 29)
    d["u"] = tiles((2 + 0.2 * rng.random((N, 128, 4, 4))) * 2.0 ** 28)
    c = 0.5 * signed(rng, N * C, 128, 4)
    b = M + rng.permutation(N * C - M)[:2 * M]
    for half, e in ((top, b[:M + M // 2]), (~top, b[M + M // 2:])):
        c[np.ix_(e, np.flatnonzero(half))] = 2.5 + 0.5 * rng.random((len(e), 64, 4))
    d["c"] = tiles(c.reshape(N, C, 128, 4).transpose(0, 2, 1, 3) * 2.0 ** 28)
    return d
def setup_inputs_low(rng):
    d = setup_inputs(rng)
    s = np.where(np.stack([rng.permutation(T) for r in range(N)]) < 3 * T // 4, 1.0, -1.0)
    d["x"] = tiles(np.exp2(2 * rng.random((N, 128, T, 4))) * s[:, None, :, None] * 2.0 ** 28)
    d["u"] = tiles((1.85 + 2 * rng.random((N, 128, 4, 4))) * 2.0 ** 28)
    d["c"] = tiles((1.9 + 2 * rng.random((N, 128, C, 4)) + 0.1 * rng.random((N, 1, C, 1))) * 2.0 ** 28)
    return d
def setup_inputs_near(rng):
    d = setup_inputs(rng)
    c, x, u = np.zeros((N, 128, C, 4)), np.zeros((N, 128, T, 4)), np.zeros((N, 128, 4, 4))
    same = signed(rng, 64, 4)
    c[:, :64] = signed(rng, N, 64, C, 4)
    c[:, 80:88] = signed(rng, N, 8, C, 4) * 2.0 ** -3
    c[:, 112, :, 0] = 40
    c[:, 120, :, 0] = 0.25
    a, e = int(rng.integers(0, N)), rng.permutation(C)[:M]
    c[a][:64, e] = same[:, None, :]
    u[:, :64, 0] = same
    u[:, 112, 0, 0] = 40
    for r in range(N):
        h = rng.permutation(T) // 4
        i = np.zeros(T)
        i[np.argsort(h, kind="stable")] = np.arange(T) % 4 == 3
        x[r, :64] = signed(rng, 64, T // 4, 4)[:, h]
        x[r, 64:72] = signed(rng, 8, T, 4) * 2.0 ** -11
        x[r, 112, :, 0] = 40
        x[r, 120, :, 0] = (1 + i) * 2.0 ** -11
    d["c"], d["x"], d["u"] = tiles(c * 2.0 ** -4), tiles(x * 2.0 ** -4), tiles(u * 2.0 ** -4)
    return d
def setup_inputs_ties(rng):
    d = setup_inputs(rng)
    c, x, u = np.zeros((N, 128, C, 4)), np.zeros((N, 128, T, 4)), np.zeros((N, 128, 4, 4))
    h = rng.permutation(N * C) // (M // 2 + 3)
    p = signed(rng, 64, int(h.max()) + 1, 4)
    u[:, :64, 0] = p[:, 0]
    for r in range(N):
        c[r, :64] = p[:, h[C * r:C * r + C]]
        g = rng.permutation(T) // 4
        x[r, :64] = signed(rng, 64, T // 4, 4)[:, g]
        x[r, 64:] = signed(rng, 64, T, 4)
    d["c"], d["x"], d["u"] = tiles(c), tiles(x), tiles(u)
    return d
def setup_inputs_spread(rng):
    return {"c": big(wide(rng, N, 128, 4 * C, cols=6)), "x": big(wide(rng, N, 128, 4 * T, cols=6)), "u": wide(rng, N, 128, 16), "w": wide(rng, N, 128, 512 * O)}
def check_inputs(d):
    b = []
    for k, low in (("c", -16), ("x", -16), ("u", -30), ("w", -30)):
        v = np.abs(d[k].astype(np.float32))
        if not (np.isfinite(v).all() and ((v == 0) | (v >= 2.0 ** low) & (v <= 2.0 ** 30)).all()): b.append("a value of " + k)
    return b
def reference(c, x, u, w):
    every = join(*[mx_ref.quantize(np.ascontiguousarray(c[q])) for q in range(N)])
    tok = [mx_ref.quantize(np.ascontiguousarray(x[r])) for r in range(N)]
    s, mark = [], []
    for r in range(N):
        s.append(np.concatenate([mx_ref.matmul(pick(every, np.arange(i, i + 128)), tok[r]) for i in range(0, N * C, 128)]) + np.float32(0))
        a = np.concatenate([u[r], np.zeros((128, 496), BF)], axis=1)
        mark.append(mx_ref.matmul(mx_ref.quantize(a), tok[r])[0] + np.float32(0))
    free, won, made = np.ones(N * C, bool), [], []
    for t in range(R):
        gain = np.zeros(N * C, int)
        for r in range(N): gain = gain + np.sum(s[r] > mark[r], axis=1)
        win = np.argsort(np.where(free, -gain, 1), kind="stable")[:M]
        free[win] = False
        named = [np.argmax(s[r][win] - mark[r], axis=1) for r in range(N)]
        v = decode(pick(every, win))
        for i in range(G):
            v = (v + decode(join(*[pick(tok[(k + i) % N], named[(k + i) % N][k:k + 1]) for k in range(M)]))) * np.float32(0.5)
        q = mx_ref.quantize(np.ascontiguousarray(v.astype(BF)))
        full = pick(q, np.concatenate([np.arange(M), np.full(128 - M, -1)]))
        for r in range(N):
            z = mx_ref.matmul(full, tok[r])[:M] + np.float32(0)
            mark[r] = np.maximum(mark[r], np.max(z, axis=0))
        won.append(win)
        made.append(q)
    q = join(*made)
    n = R * M
    y, oc, osc = np.zeros((N, 128, O * n), np.float32), np.zeros((N, 128, 4 * n), np.uint8), np.zeros((N, 16, n), np.uint8)
    sel, mk = np.zeros((N, 1, n), np.float32), np.zeros((N, 1, T), np.float32)
    for r in range(N):
        for o in range(O): y[r, :, o * n:o * n + n] = mx_ref.matmul(mx_ref.quantize(np.ascontiguousarray(cut(w[r], o))), q)
        oc[r], osc[r] = emit(q)
        sel[r, 0] = np.concatenate(won)
        mk[r, 0] = mark[r]
    return {"y": y, "oc": oc, "osc": osc, "sel": sel, "mk": mk}

@@ -1,0 +1,488 @@
+from concourse.bass import DstId, RemoteDMATransfer
+from concourse.mybir import dt, AluOpType, AxisListType, ActivationFunctionType
+
+A = AluOpType
+AF = ActivationFunctionType
+N, C, TK, M, R, G, O = 4, 32, 256, 12, 3, 3, 3
+X4, U8, BF, F32, I32, U16 = "float8_e4m3fn_x4", "uint8", "bfloat16", "float32", "int32", "uint16"
+LP = 96
+DP = 176
+
+
+def sb(n, d):
+    return ("sbuf", [128, n], d)
+
+
+SCRATCH = {
+    "ct": sb(512, BF), "xt": sb(1024, BF), "ut": sb(512, BF), "wt": sb(1536, BF), "zt": sb(512, BF),
+    "ft": sb(512, BF), "vt": sb(512, BF), "nt": sb(512, BF), "et": sb(2048, BF), "kt": sb(1024, BF),
+    "cown": sb(128, X4), "cowns": sb(128, U8), "cq": sb(128, X4), "cqs": sb(128, U8),
+    "xq": sb(384, X4), "xqs": sb(384, U8), "wq": sb(384, X4), "wqs": sb(384, U8),
+    "pq": sb(640, X4), "pqs": sb(640, U8), "fq": sb(128, X4), "fqs": sb(128, U8),
+    "nq": sb(128, X4), "nqs": sb(128, U8), "eq": sb(512, X4), "eqs": sb(512, U8),
+    "kq": sb(256, X4), "kqs": sb(256, U8), "land": sb(LP * R, X4), "lands": sb(LP * R, U8),
+    "dq": sb(128 + DP * R, X4), "dqs": sb(128 + DP * R, U8),
+    "ip": sb(8, I32), "ii": sb(8, I32), "pf": sb(8, F32), "rw": sb(16, F32), "c32": sb(128, BF), "ke": sb(128, BF),
+    "ir": sb(16, I32), "ir2": sb(16, I32), "sm": sb(8, F32), "smi": sb(8, I32), "nb": sb(4, F32),
+    "orot": sb(16, U16), "oown": sb(2, U16), "ovg": sb(4, U16), "opk": sb(4, U16),
+    "onm": sb(8, U16), "ocd": sb(8, U16),
+    "want": sb(64, F32), "ones": sb(32, F32), "nmask": sb(4, F32), "c16": sb(4, F32), "nl": sb(4, F32),
+    "tb": sb(4 * R, F32), "won": sb(4, F32), "rs": sb(128, F32), "pat": sb(96, F32),
+    "st": sb(256, F32), "srep": sb(256, F32), "mrep": sb(8 * R, F32), "zr": sb(128, F32), "zs": sb(32 * R, F32),
+    "b1": sb(256, F32), "b2": sb(256, F32), "nd": sb(256, F32), "run": sb(256, F32), "junk": sb(256, BF),
+    "junk2": sb(16, BF), "nn": sb(8, F32),
+    "gc": sb(64, BF), "gt": sb(64 * R, BF), "gland": sb(8 * N * R, BF), "own": sb(4, F32),
+    "ab": sb(8, F32), "kx": sb(128, F32), "kxt": sb(128, F32), "jr": sb(512, BF), "acc": sb(4, F32),
+    "oh": sb(128, BF), "oht": sb(128, BF), "ohr": sb(128, BF),
+    "oh2": sb(128, BF), "oht2": sb(128, BF), "ohr2": sb(128, BF), "selv": sb(4, F32),
+    "sc": sb(192, F32), "ys": sb(108, F32),
+}
+for k in range(8):
+    SCRATCH["ps%d" % k] = ("psum", [128, 512], F32)
+
+POOL = {"v": 70, "a": 25, "t": 25, "g": 10}
+SEMAPHORES = ["ldc", "ldx", "ldu", "sto", "loc", "acq", "acs"]
+for k in range(R):
+    SEMAPHORES += ["ag%d" % k, "atq%d" % k, "ats%d" % k, "ldw%d" % k]
+for q in POOL:
+    SEMAPHORES += ["%s%d" % (q, k) for k in range(POOL[q])]
+
+
+def V(name, a, b, step=1, p0=0, p1=128):
+    return (name, p0, p1, a, b, step)
+
+
+def col(name, j):
+    return V(name, j, j + 1)
+
+
+def meets(u, v):
+    if u[0] != v[0]:
+        return False
+    if u[0].startswith("ps"):
+        return True
+    if u[2] <= v[1] or v[2] <= u[1] or u[4] <= v[3] or v[4] <= u[3]:
+        return False
+    return bool(set(range(u[3], u[4], u[5])) & set(range(v[3], v[4], v[5])))
+
+
+def emit(ops, queues, T):
+    deps = []
+    for i, o in enumerate(ops):
+        d = []
+        for j in range(i):
+            e = ops[j]
+            hit = False
+            for u in o["w"]:
+                for v in e["w"] + e["r"]:
+                    if meets(u, v) and not (u[0].startswith("ps") and o["q"] == "t" and e["q"] == "t"):
+                        hit = True
+            for u in o["r"]:
+                for v in e["w"]:
+                    if meets(u, v):
+                        hit = True
+                if u[0].startswith("ps") and o["q"] != e["q"]:
+                    for v in e["r"]:
+                        if meets(u, v):
+                            hit = True
+            if hit and o["q"] is not None:
+                d.append(j)
+        deps.append(d)
+    known = dict((q, 0) for q in queues)
+    done = [0] * len(ops)
+    waits = []
+    needed = set()
+    for i, o in enumerate(ops):
+        w = []
+        if o["q"] is not None:
+            for j in reversed(deps[i]):
+                if not known[o["q"]] >> j & 1:
+                    w.append(j)
+                    needed.add(j)
+                    known[o["q"]] |= done[j]
+            done[i] = known[o["q"]] | 1 << i
+        else:
+            done[i] = 1 << i
+        waits.append(w)
+    count = dict((q, 0) for q in POOL)
+    sig = {}
+    for i, o in enumerate(ops):
+        if o["q"] is None:
+            sig[i] = o["sem"]
+            continue
+        eng = queues[o["q"]]
+        for j in reversed(waits[i]):
+            eng.wait_ge(T.sem[sig[j][0]], sig[j][1])
+        ins = o["f"]()
+        if o["sem"] is not None:
+            if o["sem"][0] is not None:
+                ins.then_inc(T.sem[o["sem"][0]], 16)
+            sig[i] = o["sem"]
+        elif i in needed:
+            q = o["q"]
+            n = count[q]
+            count[q] = n + 1
+            name = "%s%d" % (q, n % POOL[q])
+            ins.then_inc(T.sem[name], 1)
+            sig[i] = (name, n // POOL[q] + 1)
+
+
+def rank_program(g, core, T, topo):
+    r = T.rank_of(core)
+    if r is None:
+        return
+    cores = list(T.cores)
+    others = [q for q in range(N) if q != r]
+    queues = {"v": g.vector, "a": g.scalar, "t": g.tensor, "g": g, "s": g.sync}
+    ops = []
+    stores = [0]
+    sent = [0]
+
+    def ap(v):
+        if isinstance(v, tuple):
+            if v[5] == 1:
+                return T[v[0]][v[1]:v[2], v[3]:v[4]]
+            return T[v[0]][v[1]:v[2], v[3]:v[4]:v[5]]
+        return v
+
+    def views(*a):
+        return [v for v in a if isinstance(v, tuple)]
+
+    def op(q, f, rd, wr, sem=None):
+        ops.append({"q": q, "f": f, "r": rd, "w": wr, "sem": sem})
+
+    def src(v, off):
+        return ap(v) if off is None else ap(v).indirect(ap(off))
+
+    def memset(o, c):
+        op("v", lambda: g.vector.memset(ap(o), c), [], [o])
+
+    def copy(o, i, off=None):
+        op("v", lambda: g.vector.tensor_copy(ap(o), src(i, off)), views(i, off), [o])
+
+    def tt(o, i0, i1, f, off=None):
+        op("v", lambda: g.vector.tensor_tensor(ap(o), src(i0, off), ap(i1), f), views(i0, i1, off), [o])
+
+    def ts(o, i, s1, f0, s2=None, f1=None, off=None):
+        if s2 is None:
+            op("v", lambda: g.vector.tensor_scalar(ap(o), src(i, off), ap(s1), None, f0), views(i, s1, off), [o])
+        else:
+            op("v", lambda: g.vector.tensor_scalar(ap(o), src(i, off), ap(s1), ap(s2), f0, f1), views(i, s1, s2, off), [o])
+
+    def reduce(o, i, f):
+        op("v", lambda: g.vector.tensor_reduce(ap(o), ap(i), AxisListType.X, f), [i], [o])
+
+    def scan(o, d0, d1, init, f0, f1):
+        op("v", lambda: g.vector.tensor_tensor_scan(ap(o), ap(d0), ap(d1), ap(init), f0, f1), views(d0, d1, init), [o])
+
+    def transpose(o, i):
+        op("v", lambda: g.vector.transpose(ap(o), ap(i)), [i], [o])
+
+    def plane(v):
+        return (v[0] + "s",) + v[1:]
+
+    def quant(o, i):
+        op("v", lambda: g.vector.quantize_mx(ap(o), ap(plane(o)), ap(i)), [i], [o, plane(o)])
+
+    def act(o, i, f, bias=0.0, scale=1.0, acc=None):
+        op("a", lambda: g.scalar.activation(ap(o), ap(i), f, bias=ap(bias), scale=ap(scale), accum_out=ap(acc)),
+           views(i, bias, scale), views(o, acc))
+
+    def fill(o, c):
+        act(o, V("zt", 0, len(range(o[3], o[4], o[5]))), AF.Identity, c)
+
+    def pick(o, w, off):
+        op("v", lambda: g.vector.tensor_copy(ap(o).bitcast(dt.uint32), ap(w).bitcast(dt.uint32).indirect(ap(off))),
+           [w, off], [o])
+        op("a", lambda: g.scalar.activation(ap(plane(o)), ap(plane(w)).indirect(ap(off)), AF.Copy),
+           [plane(w), off], [plane(o)])
+
+    def mm(bank, n, w, x, start=True, stop=True):
+        o = V("ps%d" % bank, 0, n)
+        op("t", lambda: g.tensor.matmul_mx(ap(o), ap(w), ap(plane(w)), ap(x), ap(plane(x)), start, stop),
+           [w, plane(w), x, plane(x)], [o])
+
+    def iota(o, pattern, base, cm, small=False):
+        if small:
+            op("g", lambda: g.iota(ap(o), pattern, base, cm, allow_small_or_imprecise_dtypes=True), [], [o])
+        else:
+            op("g", lambda: g.iota(ap(o), pattern, base, cm), [], [o])
+
+    def load(q, o, i, sem, after=()):
+        op(q, lambda: queues[q].dma_start(ap(o), i), list(after), [o], (sem, 16))
+
+    def store(q, o, i, codes=False):
+        stores[0] += 16
+        op(q, lambda: queues[q].dma_start(o, ap(i).bitcast(dt.uint8) if codes else ap(i)), [i], [], ("sto", None))
+
+    def engines(q, part):
+        es = None
+        for d in range(N):
+            if d != q:
+                e = topo.engines(cores[q], cores[d])
+                es = e if es is None else [k for k in es if k in e]
+        return es if part is None else es[part::2]
+
+    def send(s, d, sem, codes=False, part=None):
+        def f():
+            ids = []
+            for q in others:
+                rid, pid, ring = topo.addr(cores[q])
+                ids.append(DstId(rid=rid, pnc=pid))
+            a, b = ap(s), ap(d)
+            if codes:
+                a, b = a.bitcast(dt.uint8), b.bitcast(dt.uint8)
+            t = RemoteDMATransfer(dst_ids=ids, dma_engine_mask=sum(1 << e for e in engines(r, part)),
+                                  remote_sem=T.sem[sem], srcs=[a], dsts=[b] * len(ids))
+            return g.remote_dma_fused([t], local_sem=T.sem["loc"])
+        sent[0] += len(engines(r, part))
+        op("g", f, [s], [], (None, None))
+
+    def arrive(vs, sem, part=None):
+        op(None, None, [], vs, (sem, sum(len(engines(q, part)) for q in others)))
+
+    def span(q):
+        ks = [k for k in range(M) if (q - k) % N < G]
+        return min(ks), max(ks) + 1
+
+    PS_S0, PS_S1, PS_Z0, PS_Z1, PS_ZR, PS_G, PS_C, PS_Y = range(8)
+    PAIR, WN = V("kq", 0, 128), V("kq", 128, 256)
+    i32, ih, j16, qq, term, hi6, lo1 = [col("pf", k) for k in range(7)]
+
+    def ps(bank, a, b, step=1):
+        return V("ps%d" % bank, a, b, step)
+
+    def xwin(s):
+        return V("xq", 32 * s, 32 * s + 128)
+
+    def pwin(base, shift):
+        return V("pq", base - shift, base - shift + 128)
+
+    def mark(t, h):
+        return col("mrep", 4 * h) if t == 0 else col("zs", 32 * (t - 1) + 16 * h + M - 1)
+
+    def load_w(o, after):
+        load("s", V("wt", 512 * o, 512 * o + 512), T.w[:, 512 * o:512 * o + 512], "ldw%d" % o, after)
+
+    def raise_marks(t, h):
+        c0 = 8 * t + 4 * h
+        act(col("mrep", c0), mark(t, h), AF.Copy)
+        tt(V("mrep", c0 + 1, c0 + 4), V("zr", 64 * h + 16 + M - 1, 64 * h + 64, 16), V("mrep", c0 - 7, c0 - 4), A.max)
+
+    load("s", V("ct", 0, 128), T.c[:, :], "ldc")
+    load("s", V("xt", 0, 1024), T.x[:, :], "ldx")
+    load("a", V("ut", 0, 16), T.u[:, :], "ldu")
+    iota(col("ip", 0), [[0, 1]], 0, 1)
+    iota(V("rw", 0, 16), [[1, 16]], 0, 0, True)
+    iota(V("ir", 0, 16), [[32, 8], [0, 2]], 8 * 32 + 31, -1)
+    iota(V("c32", 0, 128), [[1, 32], [0, 4]], 0, 0, True)
+    iota(V("nb", 0, 4), [[64, 2], [1, 2]], 0, 0, True)
+    iota(V("want", 0, 32), [[0, 2], [-2, 16]], N * C - 1, 0, True)
+
+    memset(V("ct", 128, 512), 0.0)
+    memset(V("zt", 0, 512), 0.0)
+    memset(V("ut", 16, 512), 0.0)
+    p = col("ip", 0)
+    ts(col("ii", 0), p, 31, A.bitwise_and)
+    ts(col("ii", 1), p, 1, A.logical_shift_right, 31, A.bitwise_and)
+    ts(col("ii", 2), p, 15, A.bitwise_and)
+    ts(col("ii", 3), p, 2, A.logical_shift_right, 3, A.bitwise_and)
+    ts(col("ii", 4), p, 3, A.bitwise_and)
+    ts(col("ii", 5), p, 64, A.bitwise_and)
+    ts(col("ii", 6), p, 1, A.bitwise_and)
+    act(V("kt", 0, 512), V("zt", 0, 512), AF.Copy)
+    act(V("ft", 256, 512), V("zt", 0, 256), AF.Copy)
+    act(V("nt", 0, 512), V("zt", 0, 512), AF.Copy)
+
+    quant(V("cown", 0, 128), V("ct", 0, 512))
+    send(V("cown", 0, C), V("cq", C * r, C * r + C), "acq", True, 0)
+    send(V("cowns", 0, C), V("cqs", C * r, C * r + C), "acs", False, 1)
+    iota(V("ke", 0, 128), [[1, 128]], 0, -1, True)
+    iota(V("want", 32, 64), [[0, 2], [-2, 16]], 0, 0, True)
+
+    copy(V("pf", 0, 7), V("ii", 0, 7))
+    quant(V("pq", 0, 128), V("zt", 0, 512))
+    ts(V("ir2", 0, 16), V("ir", 0, 16), 5, A.logical_shift_right, 7, A.bitwise_and)
+    ts(V("oown", 0, 2), V("rw", 0, 2), 16.0, A.mult, j16, A.add)
+    quant(V("pq", 128, 256), V("ut", 0, 512))
+    copy(V("orot", 0, 16), V("ir2", 0, 16))
+    for e in (0, 1, 6, 7):
+        memset(V("kt", e, 512, 8), 1.0)
+    quant(V("xq", 0, 256), V("xt", 0, 1024))
+    quant(V("xq", 256, 384), V("xt", 0, 512))
+    for s in range(8):
+        mm(PS_ZR, 128, xwin(s), pwin(128, 16 * s), s == 0, s == 7)
+    pick(V("cq", C * r, C * r + C), V("cown", 0, C), V("oown", 0, 2))
+    for b in range(4):
+        act(V("et", 512 * b, 512 * b + 512), V("zt", 0, 512), AF.Copy)
+    fill(V("c16", 0, 4), -16.0)
+    fill(V("ones", 0, 32), 1.0)
+    fill(V("rs", 0, 128), 0.0)
+    act(V("vt", 4 * M, 512), V("zt", 4 * M, 512), AF.Copy)
+    for e in range(4):
+        fill(V("pat", e, 96, 4), (0.0, 1.0, 0.5, 0.5)[e])
+    fill(V("rs", 0, 128, 16), -1e29)
+    for a in range(4):
+        ts(V("kt", 512 + 128 * a, 640 + 128 * a), V("c32", 0, 128), ih, A.is_equal)
+    ts(col("sm", 5), hi6, lo1, A.add)
+    ts(V("nl", 0, 4), V("nb", 0, 4), i32, A.add, i32, A.add)
+    copy(V("mrep", 0, 8), ps(PS_ZR, 0, 128, 16))
+    quant(V("kq", 0, 256), V("kt", 0, 1024))
+    copy(V("b1", 0, 256), V("mrep", 0, 8), V("orot", 0, 16))
+    ts(V("nmask", 0, 4), V("nb", 0, 4), col("sm", 5), A.is_equal, -1.0, A.mult)
+    transpose(V("b2", 0, 256), V("b1", 0, 256))
+    ts(V("tb", 0, 4), V("nl", 0, 4), -1.0 / 128, A.mult, 127.0 / 128, A.add)
+    ts(col("smi", 0), qq, term, A.add, 3.0, A.add)
+    for b in range(4):
+        ts(V("et", 513 * b, 512 * b + 512, 4), V("ke", 0, 128), 0.0, A.is_equal)
+    ts(col("smi", 1), col("smi", 0), 3, A.bitwise_and)
+
+    arrive([V("cq", C * q, C * q + C) for q in others], "acq", 0)
+    arrive([V("cqs", C * q, C * q + C) for q in others], "acs", 1)
+    load_w(0, [V("cqs", C * others[0], C * others[0] + C)])
+    mm(PS_S0, 128, xwin(0), V("cq", 0, 128))
+    mm(PS_S1, 128, xwin(4), V("cq", 0, 128))
+    mm(PS_C, 256, V("cq", 0, 128), V("xq", 0, 256))
+
+    def y_products(t):
+        for o in range(O):
+            mm(PS_Y, 128, V("wq", 128 * o, 128 * o + 128), pwin(256 + 128 * t, R * M * o + M * t),
+               t == 0 and o == 0, t == R - 1 and o == O - 1)
+
+    def store_codes(t, qs):
+        b = 256 + 128 * t
+        store(qs[0], T.oc[:, 4 * M * t:4 * M * (t + 1)], V("pq", b, b + M), True)
+        for k in range(4):
+            store(qs[1 + k], T.osc[4 * k:4 * k + 4, M * t:M * (t + 1)], V("pqs", b, b + M, 1, 32 * k, 32 * k + 4))
+
+    def by_place(n, value):
+        for b in (0, 3, 1, 2):
+            wv = V("want", 32, 64) if b == 3 else V("want", 0, 32)
+            ts(V("oh" + n, 32 * b, 32 * b + 32), wv, col("acc", b), A.is_equal, value(b), A.mult)
+        transpose(V("oht" + n, 0, 128), V("oh" + n, 0, 128))
+        scan(V("ohr" + n, 0, 128), V("oht" + n, 0, 128), V("oht" + n, 0, 128), 0.0, A.max, A.max)
+
+    for t in range(R):
+        for h in range(2):
+            s_h = ps(PS_S0 + h, 0, 128) if t == 0 else V("st", 128 * h, 128 * h + 128)
+            ts(V("ft", h, 256, 2), s_h, mark(t, h), A.is_gt)
+        quant(V("fq", 0, 128), V("ft", 0, 512))
+        mm(PS_G, 128, PAIR, V("fq", 0, 128))
+        if t > 0:
+            scan(V("zr", 0, 128), V("rs", 0, 128), ps(PS_ZR, 0, 128), 0.0, A.add, A.max)
+        copy(V("gc", 0, 64), ps(PS_G, 0, 64))
+        if t > 0:
+            raise_marks(t, 0)
+        transpose(V("gt", 64 * t, 64 * t + 64), V("gc", 0, 64))
+        gains = V("gt", 64 * t + 30, 64 * t + 34)
+        gl = [V("gland", 8 * (N * t + q), 8 * (N * t + q) + 4) for q in range(N)]
+        send(gains, gl[r], "ag%d" % t)
+
+        if t == 0:
+            tt(V("nd", 0, 256), V("b2", 0, 256), ps(PS_C, 0, 256), A.subtract)
+            act(V("st", 0, 128), ps(PS_S0, 0, 128), AF.Copy)
+            act(V("st", 128, 256), ps(PS_S1, 0, 128), AF.Copy)
+            ts(col("sm", 0), term, 0.0, A.is_equal, 4.0, A.mult)
+        else:
+            raise_marks(t, 1)
+            tt(V("own", 0, 4), gains, V("tb", 4 * t, 4 * t + 4), A.add)
+            tt(V("b1", 0, 256), V("mrep", 8 * t, 8 * t + 8), V("srep", 0, 256), A.subtract, V("orot", 0, 16))
+            transpose(V("nd", 0, 256), V("b1", 0, 256))
+        scan(V("run", 0, 256), V("nd", 0, 256), V("nd", 0, 256), 1e29, A.min, A.min)
+        act(V("junk2", 0, 16), V("run", 15, 256, 16), AF.Sign, col("run", 255), -1.0, col("nn", 0))
+        act(V("junk", 0, 256), V("run", 0, 256), AF.Sign, col("run", 255), -1.0, col("nn", 4))
+        if t == 0:
+            transpose(V("srep", 0, 256), ps(PS_C, 0, 256))
+        ts(col("nn", 1), col("nn", 0), -16.0, A.mult)
+        ts(V("nt", 0, 16, 4), V("c16", 0, 4), col("nn", 0), A.mult)
+        ts(V("nt", 1, 16, 4), V("nmask", 0, 4), col("nn", 4), A.mult, col("nn", 1), A.subtract)
+        if t == 0:
+            tt(V("own", 0, 4), gains, V("tb", 0, 4), A.add)
+        quant(V("nq", 0, 128), V("nt", 0, 512))
+        mm(PS_C, 128, WN, V("nq", 0, 128))
+        if t == 0:
+            quant(V("dq", 0, 128), V("zt", 0, 512))
+            ts(col("sm", 1), term, 47.0, A.mult, j16, A.add)
+            ts(col("sm", 3), col("smi", 1), col("sm", 0), A.max, 16.0, A.mult)
+
+        arrive([gl[q] for q in others], "ag%d" % t)
+        if t == 0:
+            load_w(1, [gl[others[0]]])
+        tt(V("ab", 0, 4), gl[others[0]], gl[others[1]], A.add)
+        tt(V("ab", 4, 8), gl[others[2]], V("own", 0, 4), A.add)
+        for b in range(2):
+            ts(V("kx", 32 * b, 32 * b + 32), V("ones", 0, 32), col("ab", b), A.mult, col("ab", 4 + b), A.add)
+        for b in range(2, 4):
+            act(V("kx", 32 * b, 32 * b + 32), V("ones", 0, 32), AF.Identity, col("ab", 4 + b), col("ab", b))
+        transpose(V("kxt", 0, 128), V("kx", 0, 128))
+        for b in range(3):
+            act(V("jr", 128 * b, 128 * b + 128), V("kxt", 0, 128), AF.Sign, col("kx", 32 * b), -1.0, col("acc", b))
+        ts(V("jr", 384, 512), V("kxt", 0, 128), col("kx", 96), A.is_gt, -2.0, A.mult)
+        reduce(col("acc", 3), V("jr", 384, 512), A.add)
+        by_place("", lambda b: ps(PS_C, b, b + 1))
+        copy(col("onm", 2 * t), col("ohr", 127))
+        lb = LP * t
+        pick(V("land", lb + 16 * r, lb + 16 * r + 16), V("xq", 0, 256), col("onm", 2 * t))
+        lo, hi = span(r)
+        mine = V("land", lb + 16 * r + lo, lb + 16 * r + hi)
+        send(mine, mine, "atq%d" % t, True)
+        send(plane(mine), plane(mine), "ats%d" % t)
+
+        by_place("2", lambda b: col("nl", b))
+        if t == 0:
+            ts(col("sm", 4), col("sm", 3), qq, A.add)
+        copy(col("ocd", 2 * t), col("ohr2", 127))
+        act(col("selv", t), col("ohr2", 127), AF.Copy)
+        quant(V("dq", DP * (t + 1), DP * (t + 1) + 128), V("zt", 0, 512))
+        pick(V("land", lb + 64, lb + 80), V("cq", 0, 128), col("ocd", 2 * t))
+        store("s", T.sel[0:1, M * t:M * (t + 1)], V("selv", t, t + 1, 1, 0, M))
+        if t == 0:
+            ts(col("sm", 2), col("sm", 1), 3.0, A.add)
+            ts(V("opk", 0, 3), V("rw", 0, 3), 4.0, A.mult, col("sm", 4), A.add)
+            quant(V("eq", 0, 512), V("et", 0, 2048))
+            ts(V("ovg", 0, 3), V("rw", 0, 3), 16.0, A.mult, col("sm", 2), A.add)
+        if t < R - 1:
+            ts(V("won", 0, 3), V("acc", 0, 3), N * C - 2.0 * M, A.is_gt, -4096.0, A.mult)
+            ts(col("won", 3), col("acc", 3), 1.0 - 2.0 * M, A.is_gt, -4096.0, A.mult)
+            tt(V("tb", 4 * t + 4, 4 * t + 8), V("tb", 4 * t, 4 * t + 4), V("won", 0, 4), A.add)
+        if t == 1:
+            quant(V("wq", 0, 384), V("wt", 0, 1536))
+            y_products(0)
+        if t == 2:
+            y_products(1)
+
+        theirs = [V("land", lb + 16 * q + span(q)[0], lb + 16 * q + span(q)[1]) for q in others]
+        arrive(theirs, "atq%d" % t)
+        arrive([plane(v) for v in theirs], "ats%d" % t)
+        if t == 0:
+            load_w(2, [plane(theirs[0])])
+        d = 128 + DP * t
+        pick(V("dq", d, d + 48), V("land", lb, lb + 80), V("opk", 0, 3))
+        for b in range(4):
+            e = d - 48 * (b % 2)
+            mm(PS_S0 + b // 2, 128, V("eq", 128 * b, 128 * b + 128), V("dq", e, e + 128), b % 2 == 0, b % 2 == 1)
+        for h in range(2):
+            scan(V("sc", 96 * h, 96 * h + 96), V("pat", 0, 96), ps(PS_S0 + h, 0, 96), 0.0, A.mult, A.add)
+        ts(V("vt", 0, 4 * M), V("sc", 0, 192), 0.5, A.mult, off=V("ovg", 0, 3))
+        b = 256 + 128 * t
+        quant(V("pq", b, b + 128), V("vt", 0, 512))
+        if t == R - 1:
+            y_products(t)
+        for h in range(2):
+            mm(PS_Z0 + h, 128, xwin(4 * h), pwin(b, 0))
+        if t < R - 1:
+            for s in (1, 2, 3, 5, 6, 7):
+                mm(PS_ZR, 128, xwin(s), pwin(b, 16 * s), s == 1, s == 7)
+        store_codes(t, "sssss" if t < R - 1 else "sssaa")
+        for h in range(2):
+            z = 32 * t + 16 * h
+            scan(V("zs", z, z + M), V("rs", 1, 1 + M), ps(PS_Z0 + h, 0, M), mark(t, h), A.add, A.max)
+
+    act(V("ys", 0, O * R * M), ps(PS_Y, 0, O * R * M), AF.Copy)
+    store("a", T.y[:, :], V("ys", 0, O * R * M))
+    for h in range(2):
+        store("sa"[h], T.mk[0:1, 128 * h:128 * h + 128], mark(R, h))
+
+    emit(ops, queues, T)
+    g.sync.wait_ge(T.sem["sto"], stores[0])
+    g.wait_ge(T.sem["loc"], sent[0])

@@ -6,41 +6,35 @@ AF = ActivationFunctionType
 N, C, TK, M, R, G, O = 4, 32, 256, 12, 3, 3, 3
 X4, U8, BF, F32, I32, U16 = "float8_e4m3fn_x4", "uint8", "bfloat16", "float32", "int32", "uint16"
 LP = 96
-DP = 176
+ZT, UT = 128, 648
+UC = 124
+CV = (256, 400, 544)
+NT, FT = 256, 272
+EQ = 144
 
 
 def sb(n, d):
     return ("sbuf", [128, n], d)
 
 
-SCRATCH = {
-    "ct": sb(512, BF), "xt": sb(1024, BF), "ut": sb(512, BF), "wt": sb(1536, BF), "zt": sb(512, BF),
-    "ft": sb(512, BF), "vt": sb(512, BF), "nt": sb(512, BF), "et": sb(2048, BF), "kt": sb(1024, BF),
-    "cown": sb(128, X4), "cowns": sb(128, U8), "cq": sb(128, X4), "cqs": sb(128, U8),
-    "xq": sb(384, X4), "xqs": sb(384, U8), "wq": sb(384, X4), "wqs": sb(384, U8),
-    "pq": sb(640, X4), "pqs": sb(640, U8), "fq": sb(128, X4), "fqs": sb(128, U8),
-    "nq": sb(128, X4), "nqs": sb(128, U8), "eq": sb(512, X4), "eqs": sb(512, U8),
-    "kq": sb(256, X4), "kqs": sb(256, U8), "land": sb(LP * R, X4), "lands": sb(LP * R, U8),
-    "dq": sb(128 + DP * R, X4), "dqs": sb(128 + DP * R, U8),
-    "ip": sb(8, I32), "ii": sb(8, I32), "pf": sb(8, F32), "rw": sb(16, F32), "c32": sb(128, BF), "ke": sb(128, BF),
-    "ir": sb(16, I32), "ir2": sb(16, I32), "sm": sb(8, F32), "smi": sb(8, I32), "nb": sb(4, F32),
-    "orot": sb(16, U16), "oown": sb(2, U16), "ovg": sb(4, U16), "opk": sb(4, U16),
-    "onm": sb(8, U16), "ocd": sb(8, U16),
-    "want": sb(64, F32), "ones": sb(32, F32), "nmask": sb(4, F32), "c16": sb(4, F32), "nl": sb(4, F32),
-    "tb": sb(4 * R, F32), "won": sb(4, F32), "rs": sb(128, F32), "pat": sb(96, F32),
-    "st": sb(256, F32), "srep": sb(256, F32), "mrep": sb(8 * R, F32), "zr": sb(128, F32), "zs": sb(32 * R, F32),
-    "b1": sb(256, F32), "b2": sb(256, F32), "nd": sb(256, F32), "run": sb(256, F32), "junk": sb(256, BF),
-    "junk2": sb(16, BF), "nn": sb(8, F32),
-    "gc": sb(64, BF), "gt": sb(64 * R, BF), "gland": sb(8 * N * R, BF), "own": sb(4, F32),
-    "ab": sb(8, F32), "kx": sb(128, F32), "kxt": sb(128, F32), "jr": sb(512, BF), "acc": sb(4, F32),
-    "oh": sb(128, BF), "oht": sb(128, BF), "ohr": sb(128, BF),
-    "oh2": sb(128, BF), "oht2": sb(128, BF), "ohr2": sb(128, BF), "selv": sb(4, F32),
-    "sc": sb(192, F32), "ys": sb(108, F32),
-}
+SCRATCH = {}
+for d, names in (
+        (BF, "zc 664 xt 1024 wt 1536 tl 528 et 520 kt 1024 sgn 128 ke 128 junk 256 junk2 16 gc 64 gt 192 "
+             "gland 560 jr 512 oh 128 oht 128 oh2 128 oht2 128"),
+        (X4, "cown 128 cq 128 xq 384 wq 384 pq 384 fq 128 nq 128 eq 656 kq 256 land 288 cv 688"),
+        (I32, "ir 16 ir2 16"),
+        (U16, "orot 16 lst 8 onm 8 ocd 8"),
+        (F32, "want 32 tab 16 nl 4 tb 12 won 4 dd 128 pat 48 st 256 srep 256 zr 416 mt 32 rt 160 rtt 160 ro 64 rot 64 "
+              "b1 256 b2 256 nd 256 run 256 nn 8 kx 140 kxt 128 acc 68 ohr 64 ohr2 64 ys 108 selv 4")):
+    names = names.split()
+    for k in range(0, len(names), 2):
+        SCRATCH[names[k]] = sb(int(names[k + 1]), d)
+        if d == X4:
+            SCRATCH[names[k] + "s"] = sb(int(names[k + 1]), U8)
 for k in range(8):
     SCRATCH["ps%d" % k] = ("psum", [128, 512], F32)
 
-POOL = {"v": 70, "a": 25, "t": 25, "g": 10}
+POOL = {"v": 60, "a": 30, "t": 25, "g": 14}
 SEMAPHORES = ["ldc", "ldx", "ldu", "sto", "loc", "acq", "acs"]
 for k in range(R):
     SEMAPHORES += ["ag%d" % k, "atq%d" % k, "ats%d" % k, "ldw%d" % k]
@@ -48,8 +42,8 @@ for q in POOL:
     SEMAPHORES += ["%s%d" % (q, k) for k in range(POOL[q])]
 
 
-def V(name, a, b, step=1, p0=0, p1=128):
-    return (name, p0, p1, a, b, step)
+def V(name, a, b, step=1, p0=0, p1=128, pstep=1):
+    return (name, p0, p1, a, b, step, pstep)
 
 
 def col(name, j):
@@ -74,7 +68,7 @@ def emit(ops, queues, T):
             e = ops[j]
             hit = False
             for u in o["w"]:
-                for v in e["w"] + e["r"]:
+                for v in e["r"] + e["w"]:
                     if meets(u, v) and not (u[0].startswith("ps") and o["q"] == "t" and e["q"] == "t"):
                         hit = True
             for u in o["r"]:
@@ -137,9 +131,12 @@ def rank_program(g, core, T, topo):
     ops = []
     stores = [0]
     sent = [0]
+    turn = col("g", 0)
 
     def ap(v):
         if isinstance(v, tuple):
+            if v[6] != 1:
+                return T[v[0]][v[1]:v[2]:v[6], v[3]:v[4]]
             if v[5] == 1:
                 return T[v[0]][v[1]:v[2], v[3]:v[4]]
             return T[v[0]][v[1]:v[2], v[3]:v[4]:v[5]]
@@ -147,6 +144,9 @@ def rank_program(g, core, T, topo):
 
     def views(*a):
         return [v for v in a if isinstance(v, tuple)]
+
+    def zeros(n, p0=0, p1=128):
+        return V("zc", ZT, ZT + n, 1, p0, p1)
 
     def op(q, f, rd, wr, sem=None):
         ops.append({"q": q, "f": f, "r": rd, "w": wr, "sem": sem})
@@ -163,14 +163,11 @@ def rank_program(g, core, T, topo):
     def tt(o, i0, i1, f, off=None):
         op("v", lambda: g.vector.tensor_tensor(ap(o), src(i0, off), ap(i1), f), views(i0, i1, off), [o])
 
-    def ts(o, i, s1, f0, s2=None, f1=None, off=None):
+    def ts(o, i, s1, f0, s2=None, f1=None):
         if s2 is None:
-            op("v", lambda: g.vector.tensor_scalar(ap(o), src(i, off), ap(s1), None, f0), views(i, s1, off), [o])
+            op("v", lambda: g.vector.tensor_scalar(ap(o), ap(i), ap(s1), None, f0), views(i, s1), [o])
         else:
-            op("v", lambda: g.vector.tensor_scalar(ap(o), src(i, off), ap(s1), ap(s2), f0, f1), views(i, s1, s2, off), [o])
-
-    def reduce(o, i, f):
-        op("v", lambda: g.vector.tensor_reduce(ap(o), ap(i), AxisListType.X, f), [i], [o])
+            op("v", lambda: g.vector.tensor_scalar(ap(o), ap(i), ap(s1), ap(s2), f0, f1), views(i, s1, s2), [o])
 
     def scan(o, d0, d1, init, f0, f1):
         op("v", lambda: g.vector.tensor_tensor_scan(ap(o), ap(d0), ap(d1), ap(init), f0, f1), views(d0, d1, init), [o])
@@ -188,32 +185,38 @@ def rank_program(g, core, T, topo):
         op("a", lambda: g.scalar.activation(ap(o), ap(i), f, bias=ap(bias), scale=ap(scale), accum_out=ap(acc)),
            views(i, bias, scale), views(o, acc))
 
-    def fill(o, c):
-        act(o, V("zt", 0, len(range(o[3], o[4], o[5]))), AF.Identity, c)
+    def gather(o, w, off):
+        op("a", lambda: g.scalar.activation(ap(o), ap(w).indirect(ap(off)), AF.Copy), [w, off], [o])
+
+    def fill(o, c=0.0):
+        act(o, zeros(len(range(o[3], o[4], o[5])), o[1], o[2]), AF.Identity, c)
 
     def pick(o, w, off):
         op("v", lambda: g.vector.tensor_copy(ap(o).bitcast(dt.uint32), ap(w).bitcast(dt.uint32).indirect(ap(off))),
            [w, off], [o])
-        op("a", lambda: g.scalar.activation(ap(plane(o)), ap(plane(w)).indirect(ap(off)), AF.Copy),
-           [plane(w), off], [plane(o)])
+        gather(plane(o), plane(w), off)
 
     def mm(bank, n, w, x, start=True, stop=True):
         o = V("ps%d" % bank, 0, n)
         op("t", lambda: g.tensor.matmul_mx(ap(o), ap(w), ap(plane(w)), ap(x), ap(plane(x)), start, stop),
            [w, plane(w), x, plane(x)], [o])
 
-    def iota(o, pattern, base, cm, small=False):
+    def iota(o, pattern, base, cm=0, small=True):
         if small:
-            op("g", lambda: g.iota(ap(o), pattern, base, cm, allow_small_or_imprecise_dtypes=True), [], [o])
+            op("g", lambda: g.iota(ap(o), pattern, base, cm, allow_small_or_imprecise_dtypes=True), [], [o, turn])
         else:
-            op("g", lambda: g.iota(ap(o), pattern, base, cm), [], [o])
+            op("g", lambda: g.iota(ap(o), pattern, base, cm), [], [o, turn])
+
+    def where_equal(o, i, pattern):
+        op("g", lambda: g.affine_select(ap(o), ap(i), pattern, A.is_equal, 0.0, 0, 1), [i], [o, turn])
 
     def load(q, o, i, sem, after=()):
         op(q, lambda: queues[q].dma_start(ap(o), i), list(after), [o], (sem, 16))
 
-    def store(q, o, i, codes=False):
+    def store(q, o, i, codes=False, after=()):
         stores[0] += 16
-        op(q, lambda: queues[q].dma_start(o, ap(i).bitcast(dt.uint8) if codes else ap(i)), [i], [], ("sto", None))
+        op(q, lambda: queues[q].dma_start(o, ap(i).bitcast(dt.uint8) if codes else ap(i)), [i] + list(after), [],
+           ("sto", None))
 
     def engines(q, part):
         es = None
@@ -223,17 +226,17 @@ def rank_program(g, core, T, topo):
                 es = e if es is None else [k for k in es if k in e]
         return es if part is None else es[part::2]
 
-    def send(s, d, sem, codes=False, part=None):
+    def send(s, ds, sem, codes=False, part=None):
         def f():
             ids = []
             for q in others:
                 rid, pid, ring = topo.addr(cores[q])
                 ids.append(DstId(rid=rid, pnc=pid))
-            a, b = ap(s), ap(d)
+            a, b = ap(s), [ap(d) for d in ds]
             if codes:
-                a, b = a.bitcast(dt.uint8), b.bitcast(dt.uint8)
+                a, b = a.bitcast(dt.uint8), [d.bitcast(dt.uint8) for d in b]
             t = RemoteDMATransfer(dst_ids=ids, dma_engine_mask=sum(1 << e for e in engines(r, part)),
-                                  remote_sem=T.sem[sem], srcs=[a], dsts=[b] * len(ids))
+                                  remote_sem=T.sem[sem], srcs=[a], dsts=b)
             return g.remote_dma_fused([t], local_sem=T.sem["loc"])
         sent[0] += len(engines(r, part))
         op("g", f, [s], [], (None, None))
@@ -245,9 +248,10 @@ def rank_program(g, core, T, topo):
         ks = [k for k in range(M) if (q - k) % N < G]
         return min(ks), max(ks) + 1
 
-    PS_S0, PS_S1, PS_Z0, PS_Z1, PS_ZR, PS_G, PS_C, PS_Y = range(8)
-    PAIR, WN = V("kq", 0, 128), V("kq", 128, 256)
-    i32, ih, j16, qq, term, hi6, lo1 = [col("pf", k) for k in range(7)]
+    PS_S0, PS_S1, PS_Z0, PS_Z1, PS_A, PS_B, PS_G, PS_C = range(8)
+    DEC = (PS_S0, PS_S1, PS_G, PS_C)
+    PAIR, WN, TILE = V("kq", 0, 128), V("kq", 128, 256), V("tl", 16, 528)
+    OPK, OCV, OWN = V("lst", 0, 3), col("lst", 4), V("lst", 6, 8)
 
     def ps(bank, a, b, step=1):
         return V("ps%d" % bank, a, b, step)
@@ -255,233 +259,230 @@ def rank_program(g, core, T, topo):
     def xwin(s):
         return V("xq", 32 * s, 32 * s + 128)
 
-    def pwin(base, shift):
-        return V("pq", base - shift, base - shift + 128)
+    def cwin(base, shift):
+        return V("cv", base - shift, base - shift + 128)
+
+    def wtile(o):
+        return V("wq", 128 * o, 128 * o + 128)
+
+    def quant_w(o):
+        quant(wtile(o), V("wt", 512 * o, 512 * o + 512))
 
     def mark(t, h):
-        return col("mrep", 4 * h) if t == 0 else col("zs", 32 * (t - 1) + 16 * h + M - 1)
+        return col("zr", 128 * t + (64 if t < R else M) * h + M - 1)
 
-    def load_w(o, after):
-        load("s", V("wt", 512 * o, 512 * o + 512), T.w[:, 512 * o:512 * o + 512], "ldw%d" % o, after)
+    def slot(t, k):
+        return V("gland", 16 * k + 4 * t, 16 * k + 4 * t + 4)
 
     def raise_marks(t, h):
-        c0 = 8 * t + 4 * h
-        act(col("mrep", c0), mark(t, h), AF.Copy)
-        tt(V("mrep", c0 + 1, c0 + 4), V("zr", 64 * h + 16 + M - 1, 64 * h + 64, 16), V("mrep", c0 - 7, c0 - 4), A.max)
+        a = 64 * h + M
+        scan(V("zr", 128 * t + a, 128 * t + a + 52), ps(PS_A + h, M, 64), V("dd", a, a + 52), 0.0, A.max, A.add)
 
-    load("s", V("ct", 0, 128), T.c[:, :], "ldc")
+    def window_products(t, h):
+        for s in (1, 2, 3):
+            mm(PS_A + h, 128, xwin(4 * h + s), cwin(CV[t], 16 * s), s == 1, s == 3)
+
+    def y_products(t):
+        for o in range(O):
+            mm(PS_A, 128, wtile(o), cwin(CV[t], R * M * o + M * t), t == 0 and o == 0, t == R - 1 and o == O - 1)
+
+    def key(b):
+        return col("kx", 8 + b if b else 108)
+
+    def by_place(n, value):
+        for b in (1, 0, 2, 3):
+            ts(V("oh" + n, 32 * b, 32 * b + 32), V("want", 0, 32), col("acc", 63 + b), A.is_equal, value(b), A.mult)
+        transpose(V("oht" + n, 0, 128), V("oh" + n, 0, 128))
+        scan(V("ohr" + n, 0, 64), V("oht" + n, 0, 64), V("oht" + n, 64, 128), 0.0, A.max, A.max)
+
+    load("s", V("zc", 0, 128), T.c[:, :], "ldc")
     load("s", V("xt", 0, 1024), T.x[:, :], "ldx")
-    load("a", V("ut", 0, 16), T.u[:, :], "ldu")
-    iota(col("ip", 0), [[0, 1]], 0, 1)
-    iota(V("rw", 0, 16), [[1, 16]], 0, 0, True)
-    iota(V("ir", 0, 16), [[32, 8], [0, 2]], 8 * 32 + 31, -1)
-    iota(V("c32", 0, 128), [[1, 32], [0, 4]], 0, 0, True)
-    iota(V("nb", 0, 4), [[64, 2], [1, 2]], 0, 0, True)
-    iota(V("want", 0, 32), [[0, 2], [-2, 16]], N * C - 1, 0, True)
-
-    memset(V("ct", 128, 512), 0.0)
-    memset(V("zt", 0, 512), 0.0)
-    memset(V("ut", 16, 512), 0.0)
-    p = col("ip", 0)
-    ts(col("ii", 0), p, 31, A.bitwise_and)
-    ts(col("ii", 1), p, 1, A.logical_shift_right, 31, A.bitwise_and)
-    ts(col("ii", 2), p, 15, A.bitwise_and)
-    ts(col("ii", 3), p, 2, A.logical_shift_right, 3, A.bitwise_and)
-    ts(col("ii", 4), p, 3, A.bitwise_and)
-    ts(col("ii", 5), p, 64, A.bitwise_and)
-    ts(col("ii", 6), p, 1, A.bitwise_and)
-    act(V("kt", 0, 512), V("zt", 0, 512), AF.Copy)
-    act(V("ft", 256, 512), V("zt", 0, 256), AF.Copy)
-    act(V("nt", 0, 512), V("zt", 0, 512), AF.Copy)
-
-    quant(V("cown", 0, 128), V("ct", 0, 512))
-    send(V("cown", 0, C), V("cq", C * r, C * r + C), "acq", True, 0)
-    send(V("cowns", 0, C), V("cqs", C * r, C * r + C), "acs", False, 1)
-    iota(V("ke", 0, 128), [[1, 128]], 0, -1, True)
-    iota(V("want", 32, 64), [[0, 2], [-2, 16]], 0, 0, True)
-
-    copy(V("pf", 0, 7), V("ii", 0, 7))
-    quant(V("pq", 0, 128), V("zt", 0, 512))
+    load("s", V("zc", UT, UT + 16), T.u[:, :], "ldu")
+    iota(V("ir", 0, 16), [[32, 8], [0, 2]], 8 * 32 + 31, -1, False)
+    iota(V("ro", 0, 64), [[16, 2], [0, 2], [1, 16]], 0)
+    memset(zeros(520), 0.0)
     ts(V("ir2", 0, 16), V("ir", 0, 16), 5, A.logical_shift_right, 7, A.bitwise_and)
-    ts(V("oown", 0, 2), V("rw", 0, 2), 16.0, A.mult, j16, A.add)
-    quant(V("pq", 128, 256), V("ut", 0, 512))
-    copy(V("orot", 0, 16), V("ir2", 0, 16))
+    quant(V("cown", 0, 128), V("zc", 0, 512))
+    own = V("cq", C * r, C * r + C)
+    send(V("cown", 0, C), [own] * 3, "acq", True, 0)
+    send(V("cowns", 0, C), [plane(own)] * 3, "acs", False, 1)
+
+    fill(V("ke", 0, 128), 0.5)
+    fill(V("et", 0, 520))
+    fill(V("zr", 0, 128))
+    fill(V("kt", 0, 512))
     for e in (0, 1, 6, 7):
-        memset(V("kt", e, 512, 8), 1.0)
+        fill(V("kt", e, 512, 8), 1.0)
+    fill(V("tl", 0, FT))
+    where_equal(V("et", 3, 515, 4), V("ke", 0, 128), [[-1, 128]])
+    iota(V("sgn", 0, 128), [[0, 64], [2, 2]], -1)
+    for h in range(2):
+        where_equal(V("kt", 512, 640, 1, 64 * h, 64 * h + 64), V("sgn", 0, 128, 1, 64 * h, 64 * h + 64),
+                    [[-2, 32], [-1, 2], [0, 2]])
+    for a in range(4):
+        iota(V("nl", 0, 4, 1, 32 * a, 32 * a + 32), [[64, 2], [1, 2]], 0, 2)
+    iota(V("want", 0, 32), [[0, 2], [-2, 16]], N * C - 1)
+
+    ts(V("orot", 0, 16), V("ir2", 0, 16), 16.0, A.mult, M - 1.0, A.add)
+    transpose(V("rot", 0, 64), V("ro", 0, 64))
+    quant(V("cv", 128, 256), zeros(512))
+    copy(OWN, V("rot", 0, 64, 32))
+    quant(V("cv", CV[0] + 16, CV[1]), zeros(512))
+    quant(V("cv", CV[1] + 16, CV[2]), zeros(512))
+    quant(V("cv", CV[2] + 16, CV[2] + 144), zeros(512))
+    pick(own, V("cown", 0, C), OWN)
     quant(V("xq", 0, 256), V("xt", 0, 1024))
+    quant(V("cv", 0, 128), V("zc", UT + 16 - 512, UT + 16))
     quant(V("xq", 256, 384), V("xt", 0, 512))
     for s in range(8):
-        mm(PS_ZR, 128, xwin(s), pwin(128, 16 * s), s == 0, s == 7)
-    pick(V("cq", C * r, C * r + C), V("cown", 0, C), V("oown", 0, 2))
+        mm(PS_A + s // 4, 128, xwin(s), cwin(UC, 16 * (s % 4)), s % 4 == 0, s % 4 == 3)
     for b in range(4):
-        act(V("et", 512 * b, 512 * b + 512), V("zt", 0, 512), AF.Copy)
-    fill(V("c16", 0, 4), -16.0)
-    fill(V("ones", 0, 32), 1.0)
-    fill(V("rs", 0, 128), 0.0)
-    act(V("vt", 4 * M, 512), V("zt", 4 * M, 512), AF.Copy)
-    for e in range(4):
-        fill(V("pat", e, 96, 4), (0.0, 1.0, 0.5, 0.5)[e])
-    fill(V("rs", 0, 128, 16), -1e29)
-    for a in range(4):
-        ts(V("kt", 512 + 128 * a, 640 + 128 * a), V("c32", 0, 128), ih, A.is_equal)
-    ts(col("sm", 5), hi6, lo1, A.add)
-    ts(V("nl", 0, 4), V("nb", 0, 4), i32, A.add, i32, A.add)
-    copy(V("mrep", 0, 8), ps(PS_ZR, 0, 128, 16))
-    quant(V("kq", 0, 256), V("kt", 0, 1024))
-    copy(V("b1", 0, 256), V("mrep", 0, 8), V("orot", 0, 16))
-    ts(V("nmask", 0, 4), V("nb", 0, 4), col("sm", 5), A.is_equal, -1.0, A.mult)
+        quant(V("eq", EQ + 128 * b, EQ + 128 * b + 128), V("et", 3 - b, 515 - b))
+        if b == 1:
+            copy(V("zr", M - 1, 64, 16), ps(PS_A, 0, 64, 16))
+    act(V("zr", 64 + M - 1, 128, 16), ps(PS_B, 0, 64, 16), AF.Copy)
+    gather(V("b1", 0, 256), V("zr", 0, 128), V("orot", 0, 16))
+    quant(PAIR, V("kt", 0, 512))
+    for a in range(1, 4):
+        act(V("kt", 512 + 128 * a, 640 + 128 * a), V("kt", 512, 640), AF.Copy)
     transpose(V("b2", 0, 256), V("b1", 0, 256))
-    ts(V("tb", 0, 4), V("nl", 0, 4), -1.0 / 128, A.mult, 127.0 / 128, A.add)
-    ts(col("smi", 0), qq, term, A.add, 3.0, A.add)
-    for b in range(4):
-        ts(V("et", 513 * b, 512 * b + 512, 4), V("ke", 0, 128), 0.0, A.is_equal)
-    ts(col("smi", 1), col("smi", 0), 3, A.bitwise_and)
+    fill(V("gland", 64, 560))
+    fill(V("tab", 0, 16))
+    act(V("tb", 0, 4), V("nl", 0, 4), AF.Identity, 127.0 / 128, -1.0 / 128)
+    fill(V("tab", 1, 8, 6, 0, 64), -1.0)
+    fill(V("tab", 9, 16, 6, 64, 128), -1.0)
 
     arrive([V("cq", C * q, C * q + C) for q in others], "acq", 0)
     arrive([V("cqs", C * q, C * q + C) for q in others], "acs", 1)
-    load_w(0, [V("cqs", C * others[0], C * others[0] + C)])
     mm(PS_S0, 128, xwin(0), V("cq", 0, 128))
     mm(PS_S1, 128, xwin(4), V("cq", 0, 128))
     mm(PS_C, 256, V("cq", 0, 128), V("xq", 0, 256))
 
-    def y_products(t):
-        for o in range(O):
-            mm(PS_Y, 128, V("wq", 128 * o, 128 * o + 128), pwin(256 + 128 * t, R * M * o + M * t),
-               t == 0 and o == 0, t == R - 1 and o == O - 1)
-
-    def store_codes(t, qs):
-        b = 256 + 128 * t
-        store(qs[0], T.oc[:, 4 * M * t:4 * M * (t + 1)], V("pq", b, b + M), True)
-        for k in range(4):
-            store(qs[1 + k], T.osc[4 * k:4 * k + 4, M * t:M * (t + 1)], V("pqs", b, b + M, 1, 32 * k, 32 * k + 4))
-
-    def by_place(n, value):
-        for b in (0, 3, 1, 2):
-            wv = V("want", 32, 64) if b == 3 else V("want", 0, 32)
-            ts(V("oh" + n, 32 * b, 32 * b + 32), wv, col("acc", b), A.is_equal, value(b), A.mult)
-        transpose(V("oht" + n, 0, 128), V("oh" + n, 0, 128))
-        scan(V("ohr" + n, 0, 128), V("oht" + n, 0, 128), V("oht" + n, 0, 128), 0.0, A.max, A.max)
-
     for t in range(R):
         for h in range(2):
             s_h = ps(PS_S0 + h, 0, 128) if t == 0 else V("st", 128 * h, 128 * h + 128)
-            ts(V("ft", h, 256, 2), s_h, mark(t, h), A.is_gt)
-        quant(V("fq", 0, 128), V("ft", 0, 512))
+            ts(V("tl", FT + h, FT + 256, 2), s_h, mark(t, h), A.is_gt)
+        quant(V("fq", 0, 128), TILE)
         mm(PS_G, 128, PAIR, V("fq", 0, 128))
         if t > 0:
-            scan(V("zr", 0, 128), V("rs", 0, 128), ps(PS_ZR, 0, 128), 0.0, A.add, A.max)
-        copy(V("gc", 0, 64), ps(PS_G, 0, 64))
-        if t > 0:
+            window_products(t - 1, 1)
             raise_marks(t, 0)
+        else:
+            quant(WN, V("kt", 512, 1024))
+        copy(V("gc", 0, 64), ps(PS_G, 64, 128))
         transpose(V("gt", 64 * t, 64 * t + 64), V("gc", 0, 64))
         gains = V("gt", 64 * t + 30, 64 * t + 34)
-        gl = [V("gland", 8 * (N * t + q), 8 * (N * t + q) + 4) for q in range(N)]
-        send(gains, gl[r], "ag%d" % t)
+        send(gains, [slot(t, r if r < q else r - 1) for q in others], "ag%d" % t)
+        act(slot(t, N - 1), gains, AF.Copy)
 
         if t == 0:
+            for e in range(4):
+                iota(V("rt", e, 96, 4), [[4, 3], [0, 2], [17 if e else 1, 4]], 16 * e - 16 if e else 64)
+            iota(V("rt", 96, 160), [[0, 4], [4, 16]], 3)
+            for e, base in ((14, 3), (11, 2), (15, 19)):
+                iota(V("rt", e, 96, 16), [[4, 3], [0, 2]], base)
             tt(V("nd", 0, 256), V("b2", 0, 256), ps(PS_C, 0, 256), A.subtract)
-            act(V("st", 0, 128), ps(PS_S0, 0, 128), AF.Copy)
-            act(V("st", 128, 256), ps(PS_S1, 0, 128), AF.Copy)
-            ts(col("sm", 0), term, 0.0, A.is_equal, 4.0, A.mult)
         else:
             raise_marks(t, 1)
-            tt(V("own", 0, 4), gains, V("tb", 4 * t, 4 * t + 4), A.add)
-            tt(V("b1", 0, 256), V("mrep", 8 * t, 8 * t + 8), V("srep", 0, 256), A.subtract, V("orot", 0, 16))
+            tt(V("b1", 0, 256), V("zr", 128 * t, 128 * t + 128), V("srep", 0, 256), A.subtract, V("orot", 0, 16))
             transpose(V("nd", 0, 256), V("b1", 0, 256))
         scan(V("run", 0, 256), V("nd", 0, 256), V("nd", 0, 256), 1e29, A.min, A.min)
-        act(V("junk2", 0, 16), V("run", 15, 256, 16), AF.Sign, col("run", 255), -1.0, col("nn", 0))
-        act(V("junk", 0, 256), V("run", 0, 256), AF.Sign, col("run", 255), -1.0, col("nn", 4))
         if t == 0:
             transpose(V("srep", 0, 256), ps(PS_C, 0, 256))
-        ts(col("nn", 1), col("nn", 0), -16.0, A.mult)
-        ts(V("nt", 0, 16, 4), V("c16", 0, 4), col("nn", 0), A.mult)
-        ts(V("nt", 1, 16, 4), V("nmask", 0, 4), col("nn", 4), A.mult, col("nn", 1), A.subtract)
-        if t == 0:
-            tt(V("own", 0, 4), gains, V("tb", 0, 4), A.add)
-        quant(V("nq", 0, 128), V("nt", 0, 512))
-        mm(PS_C, 128, WN, V("nq", 0, 128))
-        if t == 0:
-            quant(V("dq", 0, 128), V("zt", 0, 512))
-            ts(col("sm", 1), term, 47.0, A.mult, j16, A.add)
-            ts(col("sm", 3), col("smi", 1), col("sm", 0), A.max, 16.0, A.mult)
+        act(V("junk2", 0, 16), V("run", 15, 256, 16), AF.Sign, col("run", 255), -1.0, col("nn", 0))
+        act(V("junk", 0, 256), V("run", 0, 256), AF.Sign, col("run", 255), -1.0, col("nn", 4))
+        act(col("nn", 1), col("nn", 0), AF.Identity, 0.0, 16.0)
+        act(V("tl", NT, NT + 16), V("tab", 0, 16), AF.Identity, col("nn", 1), col("nn", 4))
 
-        arrive([gl[q] for q in others], "ag%d" % t)
-        if t == 0:
-            load_w(1, [gl[others[0]]])
-        tt(V("ab", 0, 4), gl[others[0]], gl[others[1]], A.add)
-        tt(V("ab", 4, 8), gl[others[2]], V("own", 0, 4), A.add)
-        for b in range(2):
-            ts(V("kx", 32 * b, 32 * b + 32), V("ones", 0, 32), col("ab", b), A.mult, col("ab", 4 + b), A.add)
-        for b in range(2, 4):
-            act(V("kx", 32 * b, 32 * b + 32), V("ones", 0, 32), AF.Identity, col("ab", 4 + b), col("ab", b))
-        transpose(V("kxt", 0, 128), V("kx", 0, 128))
-        for b in range(3):
-            act(V("jr", 128 * b, 128 * b + 128), V("kxt", 0, 128), AF.Sign, col("kx", 32 * b), -1.0, col("acc", b))
-        ts(V("jr", 384, 512), V("kxt", 0, 128), col("kx", 96), A.is_gt, -2.0, A.mult)
-        reduce(col("acc", 3), V("jr", 384, 512), A.add)
-        by_place("", lambda b: ps(PS_C, b, b + 1))
-        copy(col("onm", 2 * t), col("ohr", 127))
+        arrive([slot(t, k) for k in range(N - 1)], "ag%d" % t)
+        for b in (1, 2, 3, 0):
+            keys = V("kx", b - 1, 105, 3) if b else V("kx", 105, 140)
+            scan(keys, V("gland", 4 * t + b, 560, 16), zeros(35), col("tb", 4 * t + b), A.add, A.add)
+        transpose(V("kxt", 0, 96), V("kx", 9, 105))
+        transpose(V("kxt", 96, 128), V("kx", 108, 140))
+        quant(V("nq", 0, 128), TILE)
+        mm(PS_C, 128, WN, V("nq", 0, 128))
+        for b in range(1, 4):
+            act(V("jr", 128 * b, 128 * b + 128), V("kxt", 0, 128), AF.Sign, key(b), -1.0, col("acc", 63 + b))
+        ts(V("jr", 0, 128), V("kxt", 0, 128), key(0), A.is_gt, -2.0, A.mult)
+        scan(V("acc", 0, 64), V("jr", 0, 64), V("jr", 64, 128), N * C - 1.0, A.add, A.add)
+        by_place("", lambda b: ps(PS_C, 60 + b, 61 + b))
+        copy(col("onm", 2 * t), col("ohr", 63))
         lb = LP * t
         pick(V("land", lb + 16 * r, lb + 16 * r + 16), V("xq", 0, 256), col("onm", 2 * t))
         lo, hi = span(r)
         mine = V("land", lb + 16 * r + lo, lb + 16 * r + hi)
-        send(mine, mine, "atq%d" % t, True)
-        send(plane(mine), plane(mine), "ats%d" % t)
+        send(mine, [mine] * 3, "atq%d" % t, True)
+        send(plane(mine), [plane(mine)] * 3, "ats%d" % t)
 
+        if t < R - 1:
+            act(V("won", 0, 4), V("acc", 63, 67), AF.Relu, (2.0 * M - N * C) * 4096, 4096.0)
+        if t == 0:
+            act(V("st", 0, 128), ps(PS_S0, 0, 128), AF.Copy)
+            act(V("st", 128, 256), ps(PS_S1, 0, 128), AF.Copy)
+            for e in range(4):
+                fill(V("pat", e, 48, 4), (0.0, 1.0, 0.5, 0.5)[e])
         by_place("2", lambda b: col("nl", b))
         if t == 0:
-            ts(col("sm", 4), col("sm", 3), qq, A.add)
-        copy(col("ocd", 2 * t), col("ohr2", 127))
-        act(col("selv", t), col("ohr2", 127), AF.Copy)
-        quant(V("dq", DP * (t + 1), DP * (t + 1) + 128), V("zt", 0, 512))
-        pick(V("land", lb + 64, lb + 80), V("cq", 0, 128), col("ocd", 2 * t))
-        store("s", T.sel[0:1, M * t:M * (t + 1)], V("selv", t, t + 1, 1, 0, M))
+            transpose(V("rtt", 0, 160), V("rt", 0, 160))
+        copy(col("ocd", 2 * t), col("ohr2", 63))
         if t == 0:
-            ts(col("sm", 2), col("sm", 1), 3.0, A.add)
-            ts(V("opk", 0, 3), V("rw", 0, 3), 4.0, A.mult, col("sm", 4), A.add)
-            quant(V("eq", 0, 512), V("et", 0, 2048))
-            ts(V("ovg", 0, 3), V("rw", 0, 3), 16.0, A.mult, col("sm", 2), A.add)
-        if t < R - 1:
-            ts(V("won", 0, 3), V("acc", 0, 3), N * C - 2.0 * M, A.is_gt, -4096.0, A.mult)
-            ts(col("won", 3), col("acc", 3), 1.0 - 2.0 * M, A.is_gt, -4096.0, A.mult)
-            tt(V("tb", 4 * t + 4, 4 * t + 8), V("tb", 4 * t, 4 * t + 4), V("won", 0, 4), A.add)
+            copy(V("lst", 0, 5), V("rtt", 0, 160, 32))
+        pick(V("land", lb + 64, lb + 80), V("cq", 0, 128), col("ocd", 2 * t))
+        act(col("selv", t), col("ohr2", 63), AF.Copy)
         if t == 1:
-            quant(V("wq", 0, 384), V("wt", 0, 1536))
-            y_products(0)
+            quant_w(0)
+            quant_w(1)
         if t == 2:
+            quant_w(2)
+            y_products(0)
             y_products(1)
 
         theirs = [V("land", lb + 16 * q + span(q)[0], lb + 16 * q + span(q)[1]) for q in others]
         arrive(theirs, "atq%d" % t)
         arrive([plane(v) for v in theirs], "ats%d" % t)
-        if t == 0:
-            load_w(2, [plane(theirs[0])])
-        d = 128 + DP * t
-        pick(V("dq", d, d + 48), V("land", lb, lb + 80), V("opk", 0, 3))
-        for b in range(4):
-            e = d - 48 * (b % 2)
-            mm(PS_S0 + b // 2, 128, V("eq", 128 * b, 128 * b + 128), V("dq", e, e + 128), b % 2 == 0, b % 2 == 1)
-        for h in range(2):
-            scan(V("sc", 96 * h, 96 * h + 96), V("pat", 0, 96), ps(PS_S0 + h, 0, 96), 0.0, A.mult, A.add)
-        ts(V("vt", 0, 4 * M), V("sc", 0, 192), 0.5, A.mult, off=V("ovg", 0, 3))
-        b = 256 + 128 * t
-        quant(V("pq", b, b + 128), V("vt", 0, 512))
-        if t == R - 1:
-            y_products(t)
-        for h in range(2):
-            mm(PS_Z0 + h, 128, xwin(4 * h), pwin(b, 0))
         if t < R - 1:
-            for s in (1, 2, 3, 5, 6, 7):
-                mm(PS_ZR, 128, xwin(s), pwin(b, 16 * s), s == 1, s == 7)
-        store_codes(t, "sssss" if t < R - 1 else "sssaa")
+            a, b = 1024 * t, 1024 + 512 * t
+            load("s", V("wt", a, b), T.w[:, a:b], "ldw%d" % t, [plane(theirs[0])])
+        store("s", T.sel[0:1, M * t:M * (t + 1)], V("selv", t, t + 1, 1, 0, M), False, [theirs[0]])
+        d = 48 * (R - 1 - t)
+        pick(V("eq", d, d + 48), V("land", lb, lb + 80), OPK)
+        for b in range(4):
+            mm(DEC[b], 128, V("eq", EQ + 128 * b, EQ + 128 * b + 128), V("eq", d, d + 128))
+        if t < R - 1:
+            tt(V("tb", 4 * t + 4, 4 * t + 8), V("tb", 4 * t, 4 * t + 4), V("won", 0, 4), A.subtract)
+        if t == 0:
+            fill(V("dd", 0, 128))
+            fill(V("dd", 14, 128, 16), -1e29)
+        if t < R - 1:
+            act(V("dd", 15, 112, 16), V("zr", 128 * t + 27, 128 * t + 124, 16), AF.Copy)
+        else:
+            fill(V("zr", 128 * R + 2 * M, 128 * R + 32))
+        for b in range(4):
+            scan(V("tl", b, 192, 4), V("pat", 0, 48), ps(DEC[b], 0, 48), 0.0, A.mult, A.add)
+        made = V("pq", 128 * t, 128 * t + 128)
+        quant(made, V("tl", 0, 512))
         for h in range(2):
-            z = 32 * t + 16 * h
-            scan(V("zs", z, z + M), V("rs", 1, 1 + M), ps(PS_Z0 + h, 0, M), mark(t, h), A.add, A.max)
+            mm(PS_Z0 + h, 128, xwin(4 * h), made)
+        pick(V("cv", CV[t], CV[t] + 16), made, OCV)
+        if t < R - 1:
+            window_products(t, 0)
+        else:
+            y_products(t)
+        store("s", T.oc[:, 4 * M * t:4 * M * (t + 1)], V("cv", CV[t], CV[t] + M), True)
+        for k in range(4):
+            store("a" if t == R - 1 and k == 3 else "s", T.osc[4 * k:4 * k + 4, M * t:M * (t + 1)],
+                  V("cvs", CV[t], CV[t] + M, 1, 32 * k, 32 * k + 4))
+        for h in range(2):
+            z = mark(t + 1, h)[3] + 1 - M
+            scan(V("zr", z, z + M), zeros(M), ps(PS_Z0 + h, 3, 4 * M, 4), mark(t, h), A.add, A.max)
 
-    act(V("ys", 0, O * R * M), ps(PS_Y, 0, O * R * M), AF.Copy)
-    store("a", T.y[:, :], V("ys", 0, O * R * M))
+    transpose(V("mt", 0, 32), V("zr", 128 * R, 128 * R + 32))
+    copy(V("ys", 0, O * R * M), ps(PS_A, 0, O * R * M))
     for h in range(2):
-        store("sa"[h], T.mk[0:1, 128 * h:128 * h + 128], mark(R, h))
+        store("a", T.mk[0:1, 128 * h:128 * h + 128], V("mt", 0, 32, 1, M * h + M - 1, 128, 32))
+        if h == 0:
+            store("a", T.y[:, :], V("ys", 0, O * R * M))
 
     emit(ops, queues, T)
     g.sync.wait_ge(T.sem["sto"], stores[0])

@@ -24,8 +24,8 @@ for d, names in (
         (X4, "cown 128 cq 128 xq 384 wq 384 pq 384 fq 128 nq 128 eq 656 kq 256 land 288 cv 688"),
         (I32, "ir 16 ir2 16"),
         (U16, "orot 16 lst 8 onm 8 ocd 8"),
-        (F32, "want 32 tab 16 nl 4 tb 12 won 4 dd 128 pat 48 st 256 srep 256 zr 416 mt 32 rt 160 rtt 160 ro 64 rot 64 "
-              "b1 256 b2 256 nd 256 run 256 nn 8 kx 140 kxt 128 acc 68 ohr 64 ohr2 64 ys 108 selv 4")):
+        (F32, "want 32 tab 16 tb 12 won 4 dd 128 pat 48 st 256 zr 416 zm 48 mt 32 rt 160 rtt 160 ro 192 rot 192 "
+              "b1 256 b2 256 nd 256 run 256 nn 8 hi 16 kx 140 kxt 128 acc 68 ohr 64 ohr2 64 ys 108 selv 4")):
     names = names.split()
     for k in range(0, len(names), 2):
         SCRATCH[names[k]] = sb(int(names[k + 1]), d)
@@ -151,23 +151,20 @@ def rank_program(g, core, T, topo):
     def op(q, f, rd, wr, sem=None):
         ops.append({"q": q, "f": f, "r": rd, "w": wr, "sem": sem})
 
-    def src(v, off):
-        return ap(v) if off is None else ap(v).indirect(ap(off))
-
     def memset(o, c):
         op("v", lambda: g.vector.memset(ap(o), c), [], [o])
 
-    def copy(o, i, off=None):
-        op("v", lambda: g.vector.tensor_copy(ap(o), src(i, off)), views(i, off), [o])
+    def copy(o, i):
+        op("v", lambda: g.vector.tensor_copy(ap(o), ap(i)), [i], [o])
 
-    def tt(o, i0, i1, f, off=None):
-        op("v", lambda: g.vector.tensor_tensor(ap(o), src(i0, off), ap(i1), f), views(i0, i1, off), [o])
+    def tt(o, i0, i1, f):
+        op("v", lambda: g.vector.tensor_tensor(ap(o), ap(i0), ap(i1), f), [i0, i1], [o])
 
-    def ts(o, i, s1, f0, s2=None, f1=None):
-        if s2 is None:
-            op("v", lambda: g.vector.tensor_scalar(ap(o), ap(i), ap(s1), None, f0), views(i, s1), [o])
-        else:
-            op("v", lambda: g.vector.tensor_scalar(ap(o), ap(i), ap(s1), ap(s2), f0, f1), views(i, s1, s2), [o])
+    def ts(o, i, s1, f0, s2, f1):
+        op("v", lambda: g.vector.tensor_scalar(ap(o), ap(i), ap(s1), ap(s2), f0, f1), views(i, s1, s2), [o])
+
+    def above(o, i, s1):
+        op("v", lambda: g.vector.tensor_scalar(ap(o), ap(i), ap(s1), None, A.is_gt), [i, s1], [o])
 
     def scan(o, d0, d1, init, f0, f1):
         op("v", lambda: g.vector.tensor_tensor_scan(ap(o), ap(d0), ap(d1), ap(init), f0, f1), views(d0, d1, init), [o])
@@ -210,23 +207,25 @@ def rank_program(g, core, T, topo):
     def where_equal(o, i, pattern):
         op("g", lambda: g.affine_select(ap(o), ap(i), pattern, A.is_equal, 0.0, 0, 1), [i], [o, turn])
 
-    def load(q, o, i, sem, after=()):
-        op(q, lambda: queues[q].dma_start(ap(o), i), list(after), [o], (sem, 16))
+    def load(o, i, sem, after=()):
+        op("s", lambda: g.sync.dma_start(ap(o), i), list(after), [o], (sem, 16))
 
-    def store(q, o, i, codes=False, after=()):
+    def load_w(o, after):
+        load(V("wt", 512 * o, 512 * o + 512), T.w[:, 512 * o:512 * o + 512], "ldw%d" % o, [after])
+
+    def store(q, o, i, codes=False):
         stores[0] += 16
-        op(q, lambda: queues[q].dma_start(o, ap(i).bitcast(dt.uint8) if codes else ap(i)), [i] + list(after), [],
-           ("sto", None))
+        op(q, lambda: queues[q].dma_start(o, ap(i).bitcast(dt.uint8) if codes else ap(i)), [i], [], ("sto", None))
 
-    def engines(q, part):
+    def engines(q):
         es = None
         for d in range(N):
             if d != q:
                 e = topo.engines(cores[q], cores[d])
                 es = e if es is None else [k for k in es if k in e]
-        return es if part is None else es[part::2]
+        return es
 
-    def send(s, ds, sem, codes=False, part=None):
+    def send(s, ds, sem, codes=False):
         def f():
             ids = []
             for q in others:
@@ -235,14 +234,14 @@ def rank_program(g, core, T, topo):
             a, b = ap(s), [ap(d) for d in ds]
             if codes:
                 a, b = a.bitcast(dt.uint8), [d.bitcast(dt.uint8) for d in b]
-            t = RemoteDMATransfer(dst_ids=ids, dma_engine_mask=sum(1 << e for e in engines(r, part)),
+            t = RemoteDMATransfer(dst_ids=ids, dma_engine_mask=sum(1 << e for e in engines(r)),
                                   remote_sem=T.sem[sem], srcs=[a], dsts=b)
             return g.remote_dma_fused([t], local_sem=T.sem["loc"])
-        sent[0] += len(engines(r, part))
+        sent[0] += len(engines(r))
         op("g", f, [s], [], (None, None))
 
-    def arrive(vs, sem, part=None):
-        op(None, None, [], vs, (sem, sum(len(engines(q, part)) for q in others)))
+    def arrive(vs, sem):
+        op(None, None, [], vs, (sem, sum(len(engines(q)) for q in others)))
 
     def span(q):
         ks = [k for k in range(M) if (q - k) % N < G]
@@ -268,19 +267,26 @@ def rank_program(g, core, T, topo):
     def quant_w(o):
         quant(wtile(o), V("wt", 512 * o, 512 * o + 512))
 
+    def zero_codes(t):
+        quant(V("cv", CV[t] + 16, CV[t] + 144), zeros(512))
+
     def mark(t, h):
+        if h and 0 < t < R:
+            return col("zm", 16 * t + M - 1)
         return col("zr", 128 * t + (64 if t < R else M) * h + M - 1)
 
     def slot(t, k):
         return V("gland", 16 * k + 4 * t, 16 * k + 4 * t + 4)
 
-    def raise_marks(t, h):
-        a = 64 * h + M
-        scan(V("zr", 128 * t + a, 128 * t + a + 52), ps(PS_A + h, M, 64), V("dd", a, a + 52), 0.0, A.max, A.add)
+    def spread_marks(t):
+        for h in range(2):
+            gather(V("b1", 128 * h, 128 * h + 128), V("zr", 128 * t, 128 * t + 128), V("orot", 8 * h, 8 * h + 8))
 
-    def window_products(t, h):
-        for s in (1, 2, 3):
-            mm(PS_A + h, 128, xwin(4 * h + s), cwin(CV[t], 16 * s), s == 1, s == 3)
+    def turn_marks(h):
+        transpose(V("b2", 128 * h, 128 * h + 128), V("b1", 128 * h, 128 * h + 128))
+
+    def differences(a, b):
+        tt(V("nd", a, b), V("b2", a, b), ps(PS_B, a, b), A.subtract)
 
     def y_products(t):
         for o in range(O):
@@ -289,86 +295,86 @@ def rank_program(g, core, T, topo):
     def key(b):
         return col("kx", 8 + b if b else 108)
 
-    def by_place(n, value):
+    def by_place(n, value, between=None):
         for b in (1, 0, 2, 3):
             ts(V("oh" + n, 32 * b, 32 * b + 32), V("want", 0, 32), col("acc", 63 + b), A.is_equal, value(b), A.mult)
+        if between is not None:
+            quant_w(between)
         transpose(V("oht" + n, 0, 128), V("oh" + n, 0, 128))
         scan(V("ohr" + n, 0, 64), V("oht" + n, 0, 64), V("oht" + n, 64, 128), 0.0, A.max, A.max)
 
-    load("s", V("zc", 0, 128), T.c[:, :], "ldc")
-    load("s", V("xt", 0, 1024), T.x[:, :], "ldx")
-    load("s", V("zc", UT, UT + 16), T.u[:, :], "ldu")
+    load(V("zc", 0, 128), T.c[:, :], "ldc")
+    load(V("xt", 0, 1024), T.x[:, :], "ldx")
+    load(V("zc", UT, UT + 16), T.u[:, :], "ldu")
     iota(V("ir", 0, 16), [[32, 8], [0, 2]], 8 * 32 + 31, -1, False)
     iota(V("ro", 0, 64), [[16, 2], [0, 2], [1, 16]], 0)
+    iota(V("ke", 0, 128), [[1, 128]], 0, -1)
     memset(zeros(520), 0.0)
     ts(V("ir2", 0, 16), V("ir", 0, 16), 5, A.logical_shift_right, 7, A.bitwise_and)
     quant(V("cown", 0, 128), V("zc", 0, 512))
     own = V("cq", C * r, C * r + C)
-    send(V("cown", 0, C), [own] * 3, "acq", True, 0)
-    send(V("cowns", 0, C), [plane(own)] * 3, "acs", False, 1)
+    send(V("cown", 0, C), [own] * 3, "acq", True)
+    send(V("cowns", 0, C), [plane(own)] * 3, "acs")
 
-    fill(V("ke", 0, 128), 0.5)
-    fill(V("et", 0, 520))
     fill(V("zr", 0, 128))
     fill(V("kt", 0, 512))
     for e in (0, 1, 6, 7):
         fill(V("kt", e, 512, 8), 1.0)
-    fill(V("tl", 0, FT))
-    where_equal(V("et", 3, 515, 4), V("ke", 0, 128), [[-1, 128]])
-    iota(V("sgn", 0, 128), [[0, 64], [2, 2]], -1)
+    fill(V("et", 0, 520))
+    for e in range(2):
+        fill(V("sgn", e, 128, 2), 2.0 * e - 1)
+    iota(V("ro", 64, 192), [[64, 2], [1, 2], [2, 32]], 0)
     for h in range(2):
         where_equal(V("kt", 512, 640, 1, 64 * h, 64 * h + 64), V("sgn", 0, 128, 1, 64 * h, 64 * h + 64),
                     [[-2, 32], [-1, 2], [0, 2]])
-    for a in range(4):
-        iota(V("nl", 0, 4, 1, 32 * a, 32 * a + 32), [[64, 2], [1, 2]], 0, 2)
-    iota(V("want", 0, 32), [[0, 2], [-2, 16]], N * C - 1)
 
     ts(V("orot", 0, 16), V("ir2", 0, 16), 16.0, A.mult, M - 1.0, A.add)
     transpose(V("rot", 0, 64), V("ro", 0, 64))
     quant(V("cv", 128, 256), zeros(512))
     copy(OWN, V("rot", 0, 64, 32))
-    quant(V("cv", CV[0] + 16, CV[1]), zeros(512))
-    quant(V("cv", CV[1] + 16, CV[2]), zeros(512))
-    quant(V("cv", CV[2] + 16, CV[2] + 144), zeros(512))
+    zero_codes(0)
     pick(own, V("cown", 0, C), OWN)
     quant(V("xq", 0, 256), V("xt", 0, 1024))
     quant(V("cv", 0, 128), V("zc", UT + 16 - 512, UT + 16))
     quant(V("xq", 256, 384), V("xt", 0, 512))
     for s in range(8):
-        mm(PS_A + s // 4, 128, xwin(s), cwin(UC, 16 * (s % 4)), s % 4 == 0, s % 4 == 3)
+        mm(PS_A, 128, xwin(s), cwin(UC, 16 * s), s == 0, s == 7)
+    ts(V("et", 3, 515, 4), V("ke", 0, 128), 0.0, A.is_equal, 0.5, A.mult)
+    quant(PAIR, V("kt", 0, 512))
+    fill(V("tl", 0, FT))
     for b in range(4):
         quant(V("eq", EQ + 128 * b, EQ + 128 * b + 128), V("et", 3 - b, 515 - b))
-        if b == 1:
-            copy(V("zr", M - 1, 64, 16), ps(PS_A, 0, 64, 16))
-    act(V("zr", 64 + M - 1, 128, 16), ps(PS_B, 0, 64, 16), AF.Copy)
-    gather(V("b1", 0, 256), V("zr", 0, 128), V("orot", 0, 16))
-    quant(PAIR, V("kt", 0, 512))
-    for a in range(1, 4):
-        act(V("kt", 512 + 128 * a, 640 + 128 * a), V("kt", 512, 640), AF.Copy)
-    transpose(V("b2", 0, 256), V("b1", 0, 256))
+        if b == 2:
+            copy(V("zr", M - 1, 128, 16), ps(PS_A, 0, 128, 16))
+            spread_marks(0)
+    zero_codes(1)
     fill(V("gland", 64, 560))
+    turn_marks(0)
+    transpose(V("rot", 64, 192), V("ro", 64, 192))
     fill(V("tab", 0, 16))
-    act(V("tb", 0, 4), V("nl", 0, 4), AF.Identity, 127.0 / 128, -1.0 / 128)
     fill(V("tab", 1, 8, 6, 0, 64), -1.0)
     fill(V("tab", 9, 16, 6, 64, 128), -1.0)
+    for a in range(1, 4):
+        act(V("kt", 512 + 128 * a, 640 + 128 * a), V("kt", 512, 640), AF.Copy)
 
-    arrive([V("cq", C * q, C * q + C) for q in others], "acq", 0)
-    arrive([V("cqs", C * q, C * q + C) for q in others], "acs", 1)
+    arrive([V("cq", C * q, C * q + C) for q in others], "acq")
+    arrive([V("cqs", C * q, C * q + C) for q in others], "acs")
     mm(PS_S0, 128, xwin(0), V("cq", 0, 128))
     mm(PS_S1, 128, xwin(4), V("cq", 0, 128))
-    mm(PS_C, 256, V("cq", 0, 128), V("xq", 0, 256))
+    mm(PS_B, 256, V("cq", 0, 128), V("xq", 0, 256))
 
     for t in range(R):
         for h in range(2):
             s_h = ps(PS_S0 + h, 0, 128) if t == 0 else V("st", 128 * h, 128 * h + 128)
-            ts(V("tl", FT + h, FT + 256, 2), s_h, mark(t, h), A.is_gt)
+            above(V("tl", FT + h, FT + 256, 2), s_h, mark(t, h))
         quant(V("fq", 0, 128), TILE)
         mm(PS_G, 128, PAIR, V("fq", 0, 128))
         if t > 0:
-            window_products(t - 1, 1)
-            raise_marks(t, 0)
+            scan(V("zr", 128 * t + M, 128 * t + 128), ps(PS_A, M, 128), V("dd", M, 128), 0.0, A.max, A.add)
+            spread_marks(t)
         else:
-            quant(WN, V("kt", 512, 1024))
+            turn_marks(1)
+            act(V("tb", 0, 4), V("rot", 64, 192, 32), AF.Identity, 127.0 / 128, -1.0 / 128)
         copy(V("gc", 0, 64), ps(PS_G, 64, 128))
         transpose(V("gt", 64 * t, 64 * t + 64), V("gc", 0, 64))
         gains = V("gt", 64 * t + 30, 64 * t + 34)
@@ -376,25 +382,29 @@ def rank_program(g, core, T, topo):
         act(slot(t, N - 1), gains, AF.Copy)
 
         if t == 0:
+            iota(V("want", 0, 32), [[0, 2], [-2, 16]], N * C - 1)
             for e in range(4):
                 iota(V("rt", e, 96, 4), [[4, 3], [0, 2], [17 if e else 1, 4]], 16 * e - 16 if e else 64)
             iota(V("rt", 96, 160), [[0, 4], [4, 16]], 3)
             for e, base in ((14, 3), (11, 2), (15, 19)):
                 iota(V("rt", e, 96, 16), [[4, 3], [0, 2]], base)
-            tt(V("nd", 0, 256), V("b2", 0, 256), ps(PS_C, 0, 256), A.subtract)
+            differences(0, 256)
         else:
-            raise_marks(t, 1)
-            tt(V("b1", 0, 256), V("zr", 128 * t, 128 * t + 128), V("srep", 0, 256), A.subtract, V("orot", 0, 16))
-            transpose(V("nd", 0, 256), V("b1", 0, 256))
+            turn_marks(0)
+            turn_marks(1)
+            differences(0, 128)
+            differences(128, 256)
         scan(V("run", 0, 256), V("nd", 0, 256), V("nd", 0, 256), 1e29, A.min, A.min)
         if t == 0:
-            transpose(V("srep", 0, 256), ps(PS_C, 0, 256))
-        act(V("junk2", 0, 16), V("run", 15, 256, 16), AF.Sign, col("run", 255), -1.0, col("nn", 0))
+            quant(WN, V("kt", 512, 1024))
         act(V("junk", 0, 256), V("run", 0, 256), AF.Sign, col("run", 255), -1.0, col("nn", 4))
-        act(col("nn", 1), col("nn", 0), AF.Identity, 0.0, 16.0)
+        ts(V("hi", 0, 16), V("run", 15, 256, 16), col("run", 255), A.is_gt, -16.0, A.mult)
+        act(V("junk2", 0, 16), V("hi", 0, 16), AF.Identity, 0.0, 1.0, col("nn", 1))
         act(V("tl", NT, NT + 16), V("tab", 0, 16), AF.Identity, col("nn", 1), col("nn", 4))
 
         arrive([slot(t, k) for k in range(N - 1)], "ag%d" % t)
+        if t == 0:
+            load_w(1, slot(t, 0))
         for b in (1, 2, 3, 0):
             keys = V("kx", b - 1, 105, 3) if b else V("kx", 105, 140)
             scan(keys, V("gland", 4 * t + b, 560, 16), zeros(35), col("tb", 4 * t + b), A.add, A.add)
@@ -406,6 +416,9 @@ def rank_program(g, core, T, topo):
             act(V("jr", 128 * b, 128 * b + 128), V("kxt", 0, 128), AF.Sign, key(b), -1.0, col("acc", 63 + b))
         ts(V("jr", 0, 128), V("kxt", 0, 128), key(0), A.is_gt, -2.0, A.mult)
         scan(V("acc", 0, 64), V("jr", 0, 64), V("jr", 64, 128), N * C - 1.0, A.add, A.add)
+        if t == 0:
+            act(V("st", 0, 128), ps(PS_S0, 0, 128), AF.Copy)
+            act(V("st", 128, 256), ps(PS_S1, 0, 128), AF.Copy)
         by_place("", lambda b: ps(PS_C, 60 + b, 61 + b))
         copy(col("onm", 2 * t), col("ohr", 63))
         lb = LP * t
@@ -418,23 +431,16 @@ def rank_program(g, core, T, topo):
         if t < R - 1:
             act(V("won", 0, 4), V("acc", 63, 67), AF.Relu, (2.0 * M - N * C) * 4096, 4096.0)
         if t == 0:
-            act(V("st", 0, 128), ps(PS_S0, 0, 128), AF.Copy)
-            act(V("st", 128, 256), ps(PS_S1, 0, 128), AF.Copy)
             for e in range(4):
                 fill(V("pat", e, 48, 4), (0.0, 1.0, 0.5, 0.5)[e])
-        by_place("2", lambda b: col("nl", b))
+        by_place("2", lambda b: col("rot", 64 + 32 * b), O - 1 if t == R - 1 else None)
         if t == 0:
             transpose(V("rtt", 0, 160), V("rt", 0, 160))
         copy(col("ocd", 2 * t), col("ohr2", 63))
         if t == 0:
             copy(V("lst", 0, 5), V("rtt", 0, 160, 32))
         pick(V("land", lb + 64, lb + 80), V("cq", 0, 128), col("ocd", 2 * t))
-        act(col("selv", t), col("ohr2", 63), AF.Copy)
-        if t == 1:
-            quant_w(0)
-            quant_w(1)
-        if t == 2:
-            quant_w(2)
+        if t == R - 1:
             y_products(0)
             y_products(1)
 
@@ -442,21 +448,22 @@ def rank_program(g, core, T, topo):
         arrive(theirs, "atq%d" % t)
         arrive([plane(v) for v in theirs], "ats%d" % t)
         if t < R - 1:
-            a, b = 1024 * t, 1024 + 512 * t
-            load("s", V("wt", a, b), T.w[:, a:b], "ldw%d" % t, [plane(theirs[0])])
-        store("s", T.sel[0:1, M * t:M * (t + 1)], V("selv", t, t + 1, 1, 0, M), False, [theirs[0]])
+            load_w(2 * t, plane(theirs[0]))
         d = 48 * (R - 1 - t)
         pick(V("eq", d, d + 48), V("land", lb, lb + 80), OPK)
         for b in range(4):
             mm(DEC[b], 128, V("eq", EQ + 128 * b, EQ + 128 * b + 128), V("eq", d, d + 128))
-        if t < R - 1:
-            tt(V("tb", 4 * t + 4, 4 * t + 8), V("tb", 4 * t, 4 * t + 4), V("won", 0, 4), A.subtract)
+        act(col("selv", t), col("ohr2", 63), AF.Copy)
+        store("s", T.sel[0:1, M * t:M * (t + 1)], V("selv", t, t + 1, 1, 0, M))
         if t == 0:
             fill(V("dd", 0, 128))
             fill(V("dd", 14, 128, 16), -1e29)
         if t < R - 1:
+            tt(V("tb", 4 * t + 4, 4 * t + 8), V("tb", 4 * t, 4 * t + 4), V("won", 0, 4), A.subtract)
+            quant_w(1 - t)
             act(V("dd", 15, 112, 16), V("zr", 128 * t + 27, 128 * t + 124, 16), AF.Copy)
         else:
+            zero_codes(t)
             fill(V("zr", 128 * R + 2 * M, 128 * R + 32))
         for b in range(4):
             scan(V("tl", b, 192, 4), V("pat", 0, 48), ps(DEC[b], 0, 48), 0.0, A.mult, A.add)
@@ -466,7 +473,8 @@ def rank_program(g, core, T, topo):
             mm(PS_Z0 + h, 128, xwin(4 * h), made)
         pick(V("cv", CV[t], CV[t] + 16), made, OCV)
         if t < R - 1:
-            window_products(t, 0)
+            for s in range(1, 8):
+                mm(PS_A, 128, xwin(s), cwin(CV[t], 16 * s), s == 1, s == 7)
         else:
             y_products(t)
         store("s", T.oc[:, 4 * M * t:4 * M * (t + 1)], V("cv", CV[t], CV[t] + M), True)
@@ -474,15 +482,14 @@ def rank_program(g, core, T, topo):
             store("a" if t == R - 1 and k == 3 else "s", T.osc[4 * k:4 * k + 4, M * t:M * (t + 1)],
                   V("cvs", CV[t], CV[t] + M, 1, 32 * k, 32 * k + 4))
         for h in range(2):
-            z = mark(t + 1, h)[3] + 1 - M
-            scan(V("zr", z, z + M), zeros(M), ps(PS_Z0 + h, 3, 4 * M, 4), mark(t, h), A.add, A.max)
+            name, z = mark(t + 1, h)[0], mark(t + 1, h)[3] + 1 - M
+            scan(V(name, z, z + M), zeros(M), ps(PS_Z0 + h, 3, 4 * M, 4), mark(t, h), A.add, A.max)
 
-    transpose(V("mt", 0, 32), V("zr", 128 * R, 128 * R + 32))
     copy(V("ys", 0, O * R * M), ps(PS_A, 0, O * R * M))
+    transpose(V("mt", 0, 32), V("zr", 128 * R, 128 * R + 32))
+    store("a", T.y[:, :], V("ys", 0, O * R * M))
     for h in range(2):
-        store("a", T.mk[0:1, 128 * h:128 * h + 128], V("mt", 0, 32, 1, M * h + M - 1, 128, 32))
-        if h == 0:
-            store("a", T.y[:, :], V("ys", 0, O * R * M))
+        store("as"[h], T.mk[0:1, 128 * h:128 * h + 128], V("mt", 0, 32, 1, M * h + M - 1, 128, 32))
 
     emit(ops, queues, T)
     g.sync.wait_ge(T.sem["sto"], stores[0])

from concourse.bass import DstId, RemoteDMATransfer
from concourse.mybir import dt, AluOpType, AxisListType, ActivationFunctionType

A = AluOpType
AF = ActivationFunctionType
N, C, TK, M, R, G, O = 4, 32, 256, 12, 3, 3, 3
X4, U8, BF, F32, I32, U16 = "float8_e4m3fn_x4", "uint8", "bfloat16", "float32", "int32", "uint16"
LP = 96
ZT, UT = 128, 648
UC = 124
CV = (256, 400, 544)
NT, FT = 256, 272
EQ = 144


def sb(n, d):
    return ("sbuf", [128, n], d)


SCRATCH = {}
for d, names in (
        (BF, "zc 664 xt 1024 wt 1536 tl 528 et 520 kt 1024 sgn 128 ke 128 junk 256 junk2 16 gc 64 gt 192 "
             "gland 560 jr 512 oh 128 oht 128 oh2 128 oht2 128"),
        (X4, "cown 128 cq 128 xq 384 wq 384 pq 384 fq 128 nq 128 eq 656 kq 256 land 288 cv 688"),
        (I32, "ir 16 ir2 16"),
        (U16, "orot 16 lst 8 onm 8 ocd 8"),
        (F32, "want 32 tab 16 tb 12 won 4 dd 128 pat 48 st 256 zr 416 zm 48 mt 32 rt 160 rtt 160 ro 192 rot 192 "
              "b1 256 b2 256 nd 256 run 256 nn 8 hi 16 kx 140 kxt 128 acc 68 ohr 64 ohr2 64 ys 108 selv 4")):
    names = names.split()
    for k in range(0, len(names), 2):
        SCRATCH[names[k]] = sb(int(names[k + 1]), d)
        if d == X4:
            SCRATCH[names[k] + "s"] = sb(int(names[k + 1]), U8)
for k in range(8):
    SCRATCH["ps%d" % k] = ("psum", [128, 512], F32)

POOL = {"v": 60, "a": 30, "t": 25, "g": 14}
SEMAPHORES = ["ldc", "ldx", "ldu", "sto", "loc", "acq", "acs"]
for k in range(R):
    SEMAPHORES += ["ag%d" % k, "atq%d" % k, "ats%d" % k, "ldw%d" % k]
for q in POOL:
    SEMAPHORES += ["%s%d" % (q, k) for k in range(POOL[q])]


def V(name, a, b, step=1, p0=0, p1=128, pstep=1):
    return (name, p0, p1, a, b, step, pstep)


def col(name, j):
    return V(name, j, j + 1)


def meets(u, v):
    if u[0] != v[0]:
        return False
    if u[0].startswith("ps"):
        return True
    if u[2] <= v[1] or v[2] <= u[1] or u[4] <= v[3] or v[4] <= u[3]:
        return False
    return bool(set(range(u[3], u[4], u[5])) & set(range(v[3], v[4], v[5])))


def emit(ops, queues, T):
    deps = []
    for i, o in enumerate(ops):
        d = []
        for j in range(i):
            e = ops[j]
            hit = False
            for u in o["w"]:
                for v in e["r"] + e["w"]:
                    if meets(u, v) and not (u[0].startswith("ps") and o["q"] == "t" and e["q"] == "t"):
                        hit = True
            for u in o["r"]:
                for v in e["w"]:
                    if meets(u, v):
                        hit = True
                if u[0].startswith("ps") and o["q"] != e["q"]:
                    for v in e["r"]:
                        if meets(u, v):
                            hit = True
            if hit and o["q"] is not None:
                d.append(j)
        deps.append(d)
    known = dict((q, 0) for q in queues)
    done = [0] * len(ops)
    waits = []
    needed = set()
    for i, o in enumerate(ops):
        w = []
        if o["q"] is not None:
            for j in reversed(deps[i]):
                if not known[o["q"]] >> j & 1:
                    w.append(j)
                    needed.add(j)
                    known[o["q"]] |= done[j]
            done[i] = known[o["q"]] | 1 << i
        else:
            done[i] = 1 << i
        waits.append(w)
    count = dict((q, 0) for q in POOL)
    sig = {}
    for i, o in enumerate(ops):
        if o["q"] is None:
            sig[i] = o["sem"]
            continue
        eng = queues[o["q"]]
        for j in reversed(waits[i]):
            eng.wait_ge(T.sem[sig[j][0]], sig[j][1])
        ins = o["f"]()
        if o["sem"] is not None:
            if o["sem"][0] is not None:
                ins.then_inc(T.sem[o["sem"][0]], 16)
            sig[i] = o["sem"]
        elif i in needed:
            q = o["q"]
            n = count[q]
            count[q] = n + 1
            name = "%s%d" % (q, n % POOL[q])
            ins.then_inc(T.sem[name], 1)
            sig[i] = (name, n // POOL[q] + 1)


def rank_program(g, core, T, topo):
    r = T.rank_of(core)
    if r is None:
        return
    cores = list(T.cores)
    others = [q for q in range(N) if q != r]
    queues = {"v": g.vector, "a": g.scalar, "t": g.tensor, "g": g, "s": g.sync}
    ops = []
    stores = [0]
    sent = [0]
    turn = col("g", 0)

    def ap(v):
        if isinstance(v, tuple):
            if v[6] != 1:
                return T[v[0]][v[1]:v[2]:v[6], v[3]:v[4]]
            if v[5] == 1:
                return T[v[0]][v[1]:v[2], v[3]:v[4]]
            return T[v[0]][v[1]:v[2], v[3]:v[4]:v[5]]
        return v

    def views(*a):
        return [v for v in a if isinstance(v, tuple)]

    def zeros(n, p0=0, p1=128):
        return V("zc", ZT, ZT + n, 1, p0, p1)

    def op(q, f, rd, wr, sem=None):
        ops.append({"q": q, "f": f, "r": rd, "w": wr, "sem": sem})

    def memset(o, c):
        op("v", lambda: g.vector.memset(ap(o), c), [], [o])

    def copy(o, i):
        op("v", lambda: g.vector.tensor_copy(ap(o), ap(i)), [i], [o])

    def tt(o, i0, i1, f):
        op("v", lambda: g.vector.tensor_tensor(ap(o), ap(i0), ap(i1), f), [i0, i1], [o])

    def ts(o, i, s1, f0, s2, f1):
        op("v", lambda: g.vector.tensor_scalar(ap(o), ap(i), ap(s1), ap(s2), f0, f1), views(i, s1, s2), [o])

    def above(o, i, s1):
        op("v", lambda: g.vector.tensor_scalar(ap(o), ap(i), ap(s1), None, A.is_gt), [i, s1], [o])

    def scan(o, d0, d1, init, f0, f1):
        op("v", lambda: g.vector.tensor_tensor_scan(ap(o), ap(d0), ap(d1), ap(init), f0, f1), views(d0, d1, init), [o])

    def transpose(o, i):
        op("v", lambda: g.vector.transpose(ap(o), ap(i)), [i], [o])

    def plane(v):
        return (v[0] + "s",) + v[1:]

    def quant(o, i):
        op("v", lambda: g.vector.quantize_mx(ap(o), ap(plane(o)), ap(i)), [i], [o, plane(o)])

    def act(o, i, f, bias=0.0, scale=1.0, acc=None):
        op("a", lambda: g.scalar.activation(ap(o), ap(i), f, bias=ap(bias), scale=ap(scale), accum_out=ap(acc)),
           views(i, bias, scale), views(o, acc))

    def gather(o, w, off):
        op("a", lambda: g.scalar.activation(ap(o), ap(w).indirect(ap(off)), AF.Copy), [w, off], [o])

    def fill(o, c=0.0):
        act(o, zeros(len(range(o[3], o[4], o[5])), o[1], o[2]), AF.Identity, c)

    def pick(o, w, off):
        op("v", lambda: g.vector.tensor_copy(ap(o).bitcast(dt.uint32), ap(w).bitcast(dt.uint32).indirect(ap(off))),
           [w, off], [o])
        gather(plane(o), plane(w), off)

    def mm(bank, n, w, x, start=True, stop=True):
        o = V("ps%d" % bank, 0, n)
        op("t", lambda: g.tensor.matmul_mx(ap(o), ap(w), ap(plane(w)), ap(x), ap(plane(x)), start, stop),
           [w, plane(w), x, plane(x)], [o])

    def iota(o, pattern, base, cm=0, small=True):
        if small:
            op("g", lambda: g.iota(ap(o), pattern, base, cm, allow_small_or_imprecise_dtypes=True), [], [o, turn])
        else:
            op("g", lambda: g.iota(ap(o), pattern, base, cm), [], [o, turn])

    def where_equal(o, i, pattern):
        op("g", lambda: g.affine_select(ap(o), ap(i), pattern, A.is_equal, 0.0, 0, 1), [i], [o, turn])

    def load(o, i, sem, after=()):
        op("s", lambda: g.sync.dma_start(ap(o), i), list(after), [o], (sem, 16))

    def load_w(o, after):
        load(V("wt", 512 * o, 512 * o + 512), T.w[:, 512 * o:512 * o + 512], "ldw%d" % o, [after])

    def store(q, o, i, codes=False):
        stores[0] += 16
        op(q, lambda: queues[q].dma_start(o, ap(i).bitcast(dt.uint8) if codes else ap(i)), [i], [], ("sto", None))

    def engines(q):
        es = None
        for d in range(N):
            if d != q:
                e = topo.engines(cores[q], cores[d])
                es = e if es is None else [k for k in es if k in e]
        return es

    def send(s, ds, sem, codes=False):
        def f():
            ids = []
            for q in others:
                rid, pid, ring = topo.addr(cores[q])
                ids.append(DstId(rid=rid, pnc=pid))
            a, b = ap(s), [ap(d) for d in ds]
            if codes:
                a, b = a.bitcast(dt.uint8), [d.bitcast(dt.uint8) for d in b]
            t = RemoteDMATransfer(dst_ids=ids, dma_engine_mask=sum(1 << e for e in engines(r)),
                                  remote_sem=T.sem[sem], srcs=[a], dsts=b)
            return g.remote_dma_fused([t], local_sem=T.sem["loc"])
        sent[0] += len(engines(r))
        op("g", f, [s], [], (None, None))

    def arrive(vs, sem):
        op(None, None, [], vs, (sem, sum(len(engines(q)) for q in others)))

    def span(q):
        ks = [k for k in range(M) if (q - k) % N < G]
        return min(ks), max(ks) + 1

    PS_S0, PS_S1, PS_Z0, PS_Z1, PS_A, PS_B, PS_G, PS_C = range(8)
    DEC = (PS_S0, PS_S1, PS_G, PS_C)
    PAIR, WN, TILE = V("kq", 0, 128), V("kq", 128, 256), V("tl", 16, 528)
    OPK, OCV, OWN = V("lst", 0, 3), col("lst", 4), V("lst", 6, 8)

    def ps(bank, a, b, step=1):
        return V("ps%d" % bank, a, b, step)

    def xwin(s):
        return V("xq", 32 * s, 32 * s + 128)

    def cwin(base, shift):
        return V("cv", base - shift, base - shift + 128)

    def wtile(o):
        return V("wq", 128 * o, 128 * o + 128)

    def quant_w(o):
        quant(wtile(o), V("wt", 512 * o, 512 * o + 512))

    def zero_codes(t):
        quant(V("cv", CV[t] + 16, CV[t] + 144), zeros(512))

    def mark(t, h):
        if h and 0 < t < R:
            return col("zm", 16 * t + M - 1)
        return col("zr", 128 * t + (64 if t < R else M) * h + M - 1)

    def slot(t, k):
        return V("gland", 16 * k + 4 * t, 16 * k + 4 * t + 4)

    def spread_marks(t):
        for h in range(2):
            gather(V("b1", 128 * h, 128 * h + 128), V("zr", 128 * t, 128 * t + 128), V("orot", 8 * h, 8 * h + 8))

    def turn_marks(h):
        transpose(V("b2", 128 * h, 128 * h + 128), V("b1", 128 * h, 128 * h + 128))

    def differences(a, b):
        tt(V("nd", a, b), V("b2", a, b), ps(PS_B, a, b), A.subtract)

    def y_products(t):
        for o in range(O):
            mm(PS_A, 128, wtile(o), cwin(CV[t], R * M * o + M * t), t == 0 and o == 0, t == R - 1 and o == O - 1)

    def key(b):
        return col("kx", 8 + b if b else 108)

    def by_place(n, value, between=None):
        for b in (1, 0, 2, 3):
            ts(V("oh" + n, 32 * b, 32 * b + 32), V("want", 0, 32), col("acc", 63 + b), A.is_equal, value(b), A.mult)
        if between is not None:
            quant_w(between)
        transpose(V("oht" + n, 0, 128), V("oh" + n, 0, 128))
        scan(V("ohr" + n, 0, 64), V("oht" + n, 0, 64), V("oht" + n, 64, 128), 0.0, A.max, A.max)

    load(V("zc", 0, 128), T.c[:, :], "ldc")
    load(V("xt", 0, 1024), T.x[:, :], "ldx")
    load(V("zc", UT, UT + 16), T.u[:, :], "ldu")
    iota(V("ir", 0, 16), [[32, 8], [0, 2]], 8 * 32 + 31, -1, False)
    iota(V("ro", 0, 64), [[16, 2], [0, 2], [1, 16]], 0)
    iota(V("ke", 0, 128), [[1, 128]], 0, -1)
    memset(zeros(520), 0.0)
    ts(V("ir2", 0, 16), V("ir", 0, 16), 5, A.logical_shift_right, 7, A.bitwise_and)
    quant(V("cown", 0, 128), V("zc", 0, 512))
    own = V("cq", C * r, C * r + C)
    send(V("cown", 0, C), [own] * 3, "acq", True)
    send(V("cowns", 0, C), [plane(own)] * 3, "acs")

    fill(V("zr", 0, 128))
    fill(V("kt", 0, 512))
    for e in (0, 1, 6, 7):
        fill(V("kt", e, 512, 8), 1.0)
    fill(V("et", 0, 520))
    for e in range(2):
        fill(V("sgn", e, 128, 2), 2.0 * e - 1)
    iota(V("ro", 64, 192), [[64, 2], [1, 2], [2, 32]], 0)
    for h in range(2):
        where_equal(V("kt", 512, 640, 1, 64 * h, 64 * h + 64), V("sgn", 0, 128, 1, 64 * h, 64 * h + 64),
                    [[-2, 32], [-1, 2], [0, 2]])

    ts(V("orot", 0, 16), V("ir2", 0, 16), 16.0, A.mult, M - 1.0, A.add)
    transpose(V("rot", 0, 64), V("ro", 0, 64))
    quant(V("cv", 128, 256), zeros(512))
    copy(OWN, V("rot", 0, 64, 32))
    zero_codes(0)
    pick(own, V("cown", 0, C), OWN)
    quant(V("xq", 0, 256), V("xt", 0, 1024))
    quant(V("cv", 0, 128), V("zc", UT + 16 - 512, UT + 16))
    quant(V("xq", 256, 384), V("xt", 0, 512))
    for s in range(8):
        mm(PS_A, 128, xwin(s), cwin(UC, 16 * s), s == 0, s == 7)
    ts(V("et", 3, 515, 4), V("ke", 0, 128), 0.0, A.is_equal, 0.5, A.mult)
    quant(PAIR, V("kt", 0, 512))
    fill(V("tl", 0, FT))
    for b in range(4):
        quant(V("eq", EQ + 128 * b, EQ + 128 * b + 128), V("et", 3 - b, 515 - b))
        if b == 2:
            copy(V("zr", M - 1, 128, 16), ps(PS_A, 0, 128, 16))
            spread_marks(0)
    zero_codes(1)
    fill(V("gland", 64, 560))
    turn_marks(0)
    transpose(V("rot", 64, 192), V("ro", 64, 192))
    fill(V("tab", 0, 16))
    fill(V("tab", 1, 8, 6, 0, 64), -1.0)
    fill(V("tab", 9, 16, 6, 64, 128), -1.0)
    for a in range(1, 4):
        act(V("kt", 512 + 128 * a, 640 + 128 * a), V("kt", 512, 640), AF.Copy)

    arrive([V("cq", C * q, C * q + C) for q in others], "acq")
    arrive([V("cqs", C * q, C * q + C) for q in others], "acs")
    mm(PS_S0, 128, xwin(0), V("cq", 0, 128))
    mm(PS_S1, 128, xwin(4), V("cq", 0, 128))
    mm(PS_B, 256, V("cq", 0, 128), V("xq", 0, 256))

    for t in range(R):
        for h in range(2):
            s_h = ps(PS_S0 + h, 0, 128) if t == 0 else V("st", 128 * h, 128 * h + 128)
            above(V("tl", FT + h, FT + 256, 2), s_h, mark(t, h))
        quant(V("fq", 0, 128), TILE)
        mm(PS_G, 128, PAIR, V("fq", 0, 128))
        if t > 0:
            scan(V("zr", 128 * t + M, 128 * t + 128), ps(PS_A, M, 128), V("dd", M, 128), 0.0, A.max, A.add)
            spread_marks(t)
        else:
            turn_marks(1)
            act(V("tb", 0, 4), V("rot", 64, 192, 32), AF.Identity, 127.0 / 128, -1.0 / 128)
        copy(V("gc", 0, 64), ps(PS_G, 64, 128))
        transpose(V("gt", 64 * t, 64 * t + 64), V("gc", 0, 64))
        gains = V("gt", 64 * t + 30, 64 * t + 34)
        send(gains, [slot(t, r if r < q else r - 1) for q in others], "ag%d" % t)
        act(slot(t, N - 1), gains, AF.Copy)

        if t == 0:
            iota(V("want", 0, 32), [[0, 2], [-2, 16]], N * C - 1)
            for e in range(4):
                iota(V("rt", e, 96, 4), [[4, 3], [0, 2], [17 if e else 1, 4]], 16 * e - 16 if e else 64)
            iota(V("rt", 96, 160), [[0, 4], [4, 16]], 3)
            for e, base in ((14, 3), (11, 2), (15, 19)):
                iota(V("rt", e, 96, 16), [[4, 3], [0, 2]], base)
            differences(0, 256)
        else:
            turn_marks(0)
            turn_marks(1)
            differences(0, 128)
            differences(128, 256)
        scan(V("run", 0, 256), V("nd", 0, 256), V("nd", 0, 256), 1e29, A.min, A.min)
        if t == 0:
            quant(WN, V("kt", 512, 1024))
        act(V("junk", 0, 256), V("run", 0, 256), AF.Sign, col("run", 255), -1.0, col("nn", 4))
        ts(V("hi", 0, 16), V("run", 15, 256, 16), col("run", 255), A.is_gt, -16.0, A.mult)
        act(V("junk2", 0, 16), V("hi", 0, 16), AF.Identity, 0.0, 1.0, col("nn", 1))
        act(V("tl", NT, NT + 16), V("tab", 0, 16), AF.Identity, col("nn", 1), col("nn", 4))

        arrive([slot(t, k) for k in range(N - 1)], "ag%d" % t)
        if t == 0:
            load_w(1, slot(t, 0))
        for b in (1, 2, 3, 0):
            keys = V("kx", b - 1, 105, 3) if b else V("kx", 105, 140)
            scan(keys, V("gland", 4 * t + b, 560, 16), zeros(35), col("tb", 4 * t + b), A.add, A.add)
        transpose(V("kxt", 0, 96), V("kx", 9, 105))
        transpose(V("kxt", 96, 128), V("kx", 108, 140))
        quant(V("nq", 0, 128), TILE)
        mm(PS_C, 128, WN, V("nq", 0, 128))
        for b in range(1, 4):
            act(V("jr", 128 * b, 128 * b + 128), V("kxt", 0, 128), AF.Sign, key(b), -1.0, col("acc", 63 + b))
        ts(V("jr", 0, 128), V("kxt", 0, 128), key(0), A.is_gt, -2.0, A.mult)
        scan(V("acc", 0, 64), V("jr", 0, 64), V("jr", 64, 128), N * C - 1.0, A.add, A.add)
        if t == 0:
            act(V("st", 0, 128), ps(PS_S0, 0, 128), AF.Copy)
            act(V("st", 128, 256), ps(PS_S1, 0, 128), AF.Copy)
        by_place("", lambda b: ps(PS_C, 60 + b, 61 + b))
        copy(col("onm", 2 * t), col("ohr", 63))
        lb = LP * t
        pick(V("land", lb + 16 * r, lb + 16 * r + 16), V("xq", 0, 256), col("onm", 2 * t))
        lo, hi = span(r)
        mine = V("land", lb + 16 * r + lo, lb + 16 * r + hi)
        send(mine, [mine] * 3, "atq%d" % t, True)
        send(plane(mine), [plane(mine)] * 3, "ats%d" % t)

        if t < R - 1:
            act(V("won", 0, 4), V("acc", 63, 67), AF.Relu, (2.0 * M - N * C) * 4096, 4096.0)
        if t == 0:
            for e in range(4):
                fill(V("pat", e, 48, 4), (0.0, 1.0, 0.5, 0.5)[e])
        by_place("2", lambda b: col("rot", 64 + 32 * b), O - 1 if t == R - 1 else None)
        if t == 0:
            transpose(V("rtt", 0, 160), V("rt", 0, 160))
        copy(col("ocd", 2 * t), col("ohr2", 63))
        if t == 0:
            copy(V("lst", 0, 5), V("rtt", 0, 160, 32))
        pick(V("land", lb + 64, lb + 80), V("cq", 0, 128), col("ocd", 2 * t))
        if t == R - 1:
            y_products(0)
            y_products(1)

        theirs = [V("land", lb + 16 * q + span(q)[0], lb + 16 * q + span(q)[1]) for q in others]
        arrive(theirs, "atq%d" % t)
        arrive([plane(v) for v in theirs], "ats%d" % t)
        if t < R - 1:
            load_w(2 * t, plane(theirs[0]))
        d = 48 * (R - 1 - t)
        pick(V("eq", d, d + 48), V("land", lb, lb + 80), OPK)
        for b in range(4):
            mm(DEC[b], 128, V("eq", EQ + 128 * b, EQ + 128 * b + 128), V("eq", d, d + 128))
        act(col("selv", t), col("ohr2", 63), AF.Copy)
        store("s", T.sel[0:1, M * t:M * (t + 1)], V("selv", t, t + 1, 1, 0, M))
        if t == 0:
            fill(V("dd", 0, 128))
            fill(V("dd", 14, 128, 16), -1e29)
        if t < R - 1:
            tt(V("tb", 4 * t + 4, 4 * t + 8), V("tb", 4 * t, 4 * t + 4), V("won", 0, 4), A.subtract)
            quant_w(1 - t)
            act(V("dd", 15, 112, 16), V("zr", 128 * t + 27, 128 * t + 124, 16), AF.Copy)
        else:
            zero_codes(t)
            fill(V("zr", 128 * R + 2 * M, 128 * R + 32))
        for b in range(4):
            scan(V("tl", b, 192, 4), V("pat", 0, 48), ps(DEC[b], 0, 48), 0.0, A.mult, A.add)
        made = V("pq", 128 * t, 128 * t + 128)
        quant(made, V("tl", 0, 512))
        for h in range(2):
            mm(PS_Z0 + h, 128, xwin(4 * h), made)
        pick(V("cv", CV[t], CV[t] + 16), made, OCV)
        if t < R - 1:
            for s in range(1, 8):
                mm(PS_A, 128, xwin(s), cwin(CV[t], 16 * s), s == 1, s == 7)
        else:
            y_products(t)
        store("s", T.oc[:, 4 * M * t:4 * M * (t + 1)], V("cv", CV[t], CV[t] + M), True)
        for k in range(4):
            store("a" if t == R - 1 and k == 3 else "s", T.osc[4 * k:4 * k + 4, M * t:M * (t + 1)],
                  V("cvs", CV[t], CV[t] + M, 1, 32 * k, 32 * k + 4))
        for h in range(2):
            name, z = mark(t + 1, h)[0], mark(t + 1, h)[3] + 1 - M
            scan(V(name, z, z + M), zeros(M), ps(PS_Z0 + h, 3, 4 * M, 4), mark(t, h), A.add, A.max)

    copy(V("ys", 0, O * R * M), ps(PS_A, 0, O * R * M))
    transpose(V("mt", 0, 32), V("zr", 128 * R, 128 * R + 32))
    store("a", T.y[:, :], V("ys", 0, O * R * M))
    for h in range(2):
        store("as"[h], T.mk[0:1, 128 * h:128 * h + 128], V("mt", 0, 32, 1, M * h + M - 1, 128, 32))

    emit(ops, queues, T)
    g.sync.wait_ge(T.sem["sto"], stores[0])
    g.wait_ge(T.sem["loc"], sent[0])
